import numpy as np, ml_dtypes
CORES = [10,34,74,98]
N = 4
BF = ml_dtypes.bfloat16
def gentries(a):
    return np.ascontiguousarray(a.reshape(8, 16, -1).transpose(0, 2, 1)).reshape(8, -1)
def gtable(e):
    e = np.asarray(e); return np.ascontiguousarray(e.reshape(8, -1, 16).transpose(0, 2, 1)).reshape(128, -1).astype(np.int32)
S, A, DB, RO, MX = 2048, 4, 4, 3, 15
U = 128 >> DB
def parts(rng):
    nx = rng.integers(0, S, (N, 8, A, S))
    nx[:, 1::3] = (np.arange(S) + rng.integers(1, S // 8, nx[:, 1::3].shape)) % S
    lev = rng.random((N, 8, 16, 1), dtype=np.float32) * np.float32(0.75) + np.float32(0.25)
    rw = np.minimum(np.floor(rng.random((N, 8, 16, A * S), dtype=np.float32) * lev * np.float32(MX + 1)), np.float32(MX))
    cap = rng.integers(MX + 1, 129, (N, 8, 16, 1)); act = rng.integers(0, A, (N, 8, S))
    return nx, rw, cap, act
def pack(nx, rw, cap, act):
    return {"nx": np.stack([gtable(a.reshape(8, -1)) for a in nx]), "rw": np.ascontiguousarray(rw).reshape(N, 128, A * S).astype(np.float32).astype(BF),
            "cap": np.ascontiguousarray(cap).reshape(N, 128, 1).astype(np.float32), "act0": np.stack([gtable(a) for a in act])}
def stage(rng, nx, rw, cap, g, to, rew):
    cap[:, g] = 128
    for p in range(N):
        z, e, f = [int(v) for v in rng.permutation(S)[:3]]
        nx[p, g] = np.array([z, e, f])[to[p]]
        nx[p, g, :, z] = z; nx[p, g, :, e] = f; nx[p, g, :, f] = f
        rew[p, :, :, z] = 0; rew[p, :, :, e] = 0; rew[p, :, :, f] = U
    rw[:, g] = rew.reshape(N, 16, A * S)
def swing(rng):
    to = np.where(rng.random(S) < 0.4, 2 * rng.integers(0, 2, (1, A, S)), rng.integers(0, 3, (N, A, S)))
    rew = rng.integers(0, MX + 1, (N, 16, A, S)) * (rng.random(S) < 0.5)
    return to, rew
def brim(rng):
    to = 1 + (rng.random((N, A, S)) < 0.3).astype(np.int64)
    short = rng.random((N, 16, A, S)) * (16 * N) < 1
    return to, np.where(short, U - 1, rng.integers(U, MX + 1, short.shape))
def tug(rng):
    h = N // 2; o = rng.permutation(N); p, q = o[:h], o[h:2 * h]
    low = rng.integers(0, U + 1, (h, 16, A, S)) * (rng.random(S) < 0.7)
    high = U - low.reshape(16 * h, A, S)[rng.permutation(16 * h)].reshape(low.shape)
    b = rng.random((h, A, S)) < 0.5
    to = np.zeros((N, A, S), np.int64); rew = np.zeros((N, 16, A, S), np.int64)
    to[p] = np.where(b, 1, 0); to[q] = np.where(b, 0, 1)
    rew[p] = np.where(b[:, None], high, low); rew[q] = np.where(b[:, None], low, high)
    x = rng.random(rew.shape) * (16 * N)
    rew = rew + (x < 0.5).astype(np.int64) - (x > 16 * N - 0.5).astype(np.int64)
    return to, np.minimum(np.maximum(rew, 0), MX)
def setup_inputs(rng):
    return pack(*parts(rng))
def setup_inputs_ties(rng):
    nx, rw, cap, act = parts(rng); w = rw.reshape(N, 8, 16, A, S)
    nx[:, 0::4, 1:] = nx[:, 0::4, :1]; w[:, 0::4, :, 1:] = w[:, 0::4, :, :1]
    for g in (1, 5):
        m = rng.random(S) < 0.5
        nx[:, g] = np.where(m, nx[:, g, :1], nx[:, g]); w[:, g] = np.where(m, w[:, g, :, :1], w[:, g])
    for g in (2, 6):
        nx[:, g, 1:] = nx[:, g, :1]; cap[:, g] = 128
        w[:, g] = (4 * (rng.random((N, 16, 1, S)) < 0.3)).astype(np.float32)
        q = int(rng.integers(0, N)); i = int(rng.integers(0, 16))
        w[q, g, i] = 1; w[q, g, i, A - 1] = rng.integers(0, 3, S)
    for g in (3, 7):
        w[:, g] = MX * (rng.random((N, 16, A, S)) < 0.3).astype(np.float32); cap[:, g] = MX + 1
    return pack(nx, w, cap, act)
def setup_inputs_full(rng):
    nx, rw, cap, act = parts(rng)
    v = rng.integers(1, MX + 1, (N, 8, 16, 1))
    rw = np.where(rng.random(rw.shape, dtype=np.float32) < 0.03, rw, v.astype(np.float32))
    near = v * 2 ** DB + rng.integers(-1, 2, v.shape); ends = rng.choice(np.array([MX + 1, MX + 2, 127, 128]), v.shape)
    cap = np.minimum(np.maximum(np.where(rng.random(v.shape) < 0.6, near, ends), MX + 1), 128)
    rw[:, 0] = MX; rw[:, 1] = np.where(rng.random(rw[:, 1].shape) < 0.01, 1 + rng.integers(0, MX, rw[:, 1].shape), 0)
    return pack(nx, rw, cap, act)
def setup_inputs_chains(rng):
    nx, rw, cap, act = parts(rng); s = np.arange(S); a = np.arange(A)[:, None]
    nx[:, 0] = s; nx[:, 1] = np.minimum(s + 1 + a, S - 1); nx[:, 2] = (s - 1 - a) % S
    nx[:, 3] = rng.integers(0, S, (N, A, 1)); nx[:, 4] = np.argsort(rng.random((N, A, S)), axis=-1)
    nx[:, 5] = (S - 1) * rng.integers(0, 2, (N, A, S)); nx[:, 6, ::2] = s ^ 1; nx[:, 7] = nx[:1, 7]
    act[:, 1] = 0; act[:, 2] = A - 1; act[:, 4] = act[:1, 4]
    return pack(nx, rw, cap, act)
def setup_inputs_loud(rng):
    nx, rw, cap, act = parts(rng); o = rng.permutation(N); big = np.zeros((N, 8, 1, 1), bool)
    for g in range(8): big[o[g % N], g] = True
    big[:, 2] = True
    rw = np.where(big | (rng.random(rw.shape, dtype=np.float32) < 0.01), rw, np.float32(0))
    rw[o[0], 2] = 0; rw[:, 3] = 0
    for p in range(N):
        if not big[p, 7, 0, 0]: rw[p, 7] = 0
    for g, make in ((1, swing), (5, brim), (6, tug)):
        to, rew = make(rng); stage(rng, nx, rw, cap, g, to, rew)
    return pack(nx, rw, cap, act)
def setup_inputs_spread(rng):
    nx, rw, cap, act = parts(rng)
    e = np.exp2(rng.integers(-2, 3, (N, 8, 16, 1)) + rng.integers(-2, 3, (N, 8, 1, A * S))).astype(np.float32)
    rw = np.minimum(np.floor(np.float32(MX + 1) * rng.random(rw.shape, dtype=np.float32) ** e), np.float32(MX))
    nx = np.minimum(np.floor(S * rng.random(nx.shape) ** np.exp2(rng.integers(-2, 3, (N, 8, 1, 1)))).astype(np.int64), S - 1)
    cap = np.minimum(np.floor((MX + 1) * np.exp2(rng.random(cap.shape) * np.log2(128 / (MX + 1)) * 1.02)).astype(np.int64), 128)
    act = np.minimum(np.floor(A * rng.random(act.shape) ** 3).astype(np.int64), A - 1)
    return pack(nx, rw, cap, act)
def check_inputs(d):
    bad = []
    for k, lo, hi in (("nx", 0, S - 1), ("rw", 0, MX), ("cap", MX + 1, 128), ("act0", 0, A - 1)):
        v = np.asarray(d[k]).astype(np.float32)
        if not np.all((v >= lo) & (v <= hi) & (v == np.floor(v))): bad.append("range of " + k)
    return bad
def reference(nx, rw, cap, act0):
    n = np.stack([gentries(a) for a in nx]).astype(np.int64).reshape(N, 8, A, S)
    w = rw.astype(np.float32).astype(np.int32).reshape(N, 8, 16, A, S); c = cap.astype(np.int32).reshape(N, 8, 16, 1)
    act = np.stack([gentries(a) for a in act0]).astype(np.int64)
    for rnd in range(RO):
        t = np.take_along_axis(n, act[:, :, None, :], 2)[:, :, 0]
        r = np.take_along_axis(w, act[:, :, None, None, :], 3)[:, :, :, 0]
        for k in range(DB):
            r = np.minimum(r + np.take_along_axis(r, t[:, :, None, :], 3), c)
            t = np.take_along_axis(t, t, 2)
        q = np.zeros((8, A, S), np.int64)
        for p in range(N):
            for a in range(A):
                v = w[p][:, :, a] + np.take_along_axis(r[p], n[p][:, a][:, None, :], 2)
                q[:, a] += np.add.reduce(np.minimum(v, c[p]), axis=1)
        best = np.argmax(q, axis=1)
        act = np.stack([best for p in range(N)])
    return {"yr": r.reshape(N, 128, S).astype(np.float32).astype(BF), "ya": np.stack([gtable(a) for a in act]).astype(np.float32)}

@@ -1,0 +1,400 @@
+from concourse.bass import DstId, RemoteDMATransfer
+from concourse.mybir import AluOpType as A, ActivationFunctionType as F
+
+RO = 3
+BF, F32, I32, U16, F16 = "bfloat16", "float32", "int32", "uint16", "float16"
+SCRATCH = {n: ("sbuf", [128, w], d) for n, w, d in [
+    ("nx32", 512, I32), ("nxh", 512, F16), ("nxu", 512, U16), ("act32", 128, I32), ("capc", 4, F32), ("cols", 32, F32),
+    ("pint", 8, I32), ("rws", 8192, BF), ("nxrow", 8192, F32), ("ybuf", 8192, BF), ("gbuf", 3584, BF),
+    ("ta", 2048, BF), ("tb", 2048, BF), ("da", 2048, BF), ("db", 2048, BF), ("dc", 2048, BF), ("yrs", 2048, BF),
+    ("lists", 640, U16), ("zeros", 1024, BF), ("bmat", 2048, BF), ("g16", 128, BF), ("colmat", 16, F32), ("xrow", 144, F32),
+    ("mtile", 128, F32), ("zmat", 144, BF), ("sel", 8, BF), ("ident", 128, BF), ("nident", 128, BF), ("prm", 128, BF),
+    ("reset", 256, BF), ("kc1", 512, BF), ("kc2", 256, BF), ("ones", 128, BF), ("sumrw", 512, F32), ("tmpf", 256, F32),
+    ("scan", 512, F32), ("ki", 128, I32), ("km", 128, I32), ("yas", 128, F32), ("land", RO * 2 * 4 * 256, F16)]}
+SCRATCH.update({n: ("psum", [128, 512], F32) for n in ("x0", "x1", "x2", "x3", "s0", "s1", "e0", "e1")})
+SEMAPHORES = ["cv", "cs", "cp", "cg", "ldnx", "ldrw", "ldact", "ldcap", "st", "sent", "sh0", "sh1", "sh2", "sh3"] + [
+    "arr%d%d" % (r, h) for r in range(RO) for h in range(2)]
+
+
+def rank_program(g, core, T, topo):
+    rank = T.rank_of(core)
+    if rank is None:
+        return
+    N = len(T.cores)
+    Q = {"g": g, "v": g.vector, "s": g.scalar, "p": g.tensor, "y": g.sync}
+    CS = {"g": "cg", "v": "cv", "s": "cs", "p": "cp"}
+    count = {}
+    known = {e: {} for e in Q}
+    lastw = {}
+    readers = {}
+
+    def wait(e, tok):
+        sem, val, clock = tok[0], tok[1], tok[3]
+        if known[e].get(sem, 0) >= val:
+            return
+        Q[e].wait_ge(T.sem[sem], val)
+        known[e][sem] = val
+        for k, v in clock.items():
+            if known[e].get(k, 0) < v:
+                known[e][k] = v
+
+    def op(e, fn, reads=(), writes=(), banks=(), extra=(), sem=None, inc=1):
+        deps = list(extra)
+        for k in reads:
+            if k in lastw:
+                deps.append(lastw[k])
+        for k in writes:
+            if k in lastw:
+                deps.append(lastw[k])
+            deps.extend(readers.get(k, []))
+        for k in banks:
+            if k in lastw and lastw[k][2] != e:
+                deps.append(lastw[k])
+        best = {}
+        for t in deps:
+            if e == "p" and t[2] == "p":
+                continue
+            if t[0] not in best or best[t[0]][1] < t[1]:
+                best[t[0]] = t
+        for t in sorted(best.values(), key=lambda t: -len(t[3])):
+            wait(e, t)
+        ins = fn()
+        s = sem or CS[e]
+        count[s] = count.get(s, 0) + inc
+        if ins is not None:
+            ins.then_inc(T.sem[s], inc)
+        tok = (s, count[s], e, dict(known[e]))
+        for k in reads:
+            readers.setdefault(k, []).append(tok)
+        for k in list(writes) + list(banks):
+            lastw[k] = tok
+            readers[k] = []
+        return tok
+
+    def K(name, lo, hi):
+        return ["%s%d" % (name, j) for j in range(lo // 512, (hi + 511) // 512)]
+
+    V, S, P = g.vector, g.scalar, g.tensor
+    icol, cj, zcol, cap16 = T.cols[:, 4:5], T.cols[:, 8:9], T.cols[:, 12:13], T.cols[:, 16:17]
+    cap = T.capc[:, 0:1]
+    NXROW = ["nxrow%d" % i for i in range(16)]
+
+    op("y", lambda: g.sync.dma_start(T.nx32[:], T.nx[:]), writes=["nx32"], sem="ldnx", inc=16)
+    op("y", lambda: g.sync.dma_start(T.rws[:], T.rw[:]), writes=["rws"], sem="ldrw", inc=16)
+    op("s", lambda: S.dma_start(T.act32[:], T.act0[:]), writes=["act32"], sem="ldact", inc=16)
+    op("s", lambda: S.dma_start(cap, T.cap[:]), writes=["cap"], sem="ldcap", inc=16)
+
+    def iota(out, key, pattern, base, cm, flag=True):
+        if flag:
+            op("g", lambda: g.iota(out, pattern, base, cm, allow_small_or_imprecise_dtypes=True), writes=[key])
+        else:
+            op("g", lambda: g.iota(out, pattern, base, cm), writes=[key])
+
+    def mark(out, key, n, pattern, fill, base, cm):
+        op("g", lambda: g.affine_select(out, T.zeros[:, 0:n], pattern, A.not_equal, fill, base, cm),
+           reads=["zeros"], writes=[key])
+
+    op("v", lambda: V.memset(T.zeros[:], 0.0), writes=["zeros"])
+    iota(T.colmat[:], "colmat", [[-1, 16]], 0, 1)
+    iota(T.g16[:], "g16", [[16, 8], [0, 16]], 0, 0)
+    iota(T.pint[:, 0:1], "pint", [[0, 1]], 0, 1, False)
+    iota(T.xrow[:], "xrow", [[1, 144]], 0, 0)
+    mark(T.bmat[:, 1024:2048], "bm_hi", 1024, [[-1, 8], [-16, 8], [0, 16]], 1.0, -8, 1)
+    iota(T.mtile[:], "mtile", [[16, 128]], 0, 0)
+    for i in range(8):
+        op("v", lambda: V.tensor_scalar(T.bmat[:, 128 * i:128 * i + 128], T.g16[:], T.colmat[:, i:i + 1], None, A.is_equal),
+           reads=["g16", "colmat"], writes=["bm%d" % i])
+    op("v", lambda: V.tensor_scalar(T.pint[:, 4:5], T.pint[:, 0:1], 15, None, A.bitwise_and), reads=["pint"], writes=["pi"])
+    op("v", lambda: V.tensor_copy(icol, T.pint[:, 4:5]), reads=["pi"], writes=["icol"])
+    op("v", lambda: V.tensor_scalar(cj, T.pint[:, 4:5], 2040.5, None, A.add), reads=["pi"], writes=["cj"])
+    op("v", lambda: V.tensor_scalar(zcol, T.colmat[:, 0:1], icol, 15.0, A.subtract, A.add), reads=["colmat", "icol"], writes=["zcol"])
+    op("v", lambda: V.tensor_scalar(T.zmat[:], T.xrow[:], zcol, 0.0625, A.is_equal, A.mult), reads=["xrow", "zcol"], writes=["zmat"])
+    op("v", lambda: V.tensor_scalar(T.sel[:], T.xrow[:, 15:128:16], zcol, None, A.is_equal), reads=["xrow", "zcol"], writes=["sel"])
+    op("v", lambda: V.tensor_copy(T.nxh[:], T.nx32[:]), reads=["nx32"], writes=["nxh"])
+    mark(T.ident[:], "ident", 128, [[-1, 128]], 1.0, 0, 1)
+    mark(T.nident[:], "nident", 128, [[-1, 128]], -1.0, 0, 1)
+    mark(T.prm[:], "prm", 128, [[1, 64], [64, 2]], 8192.0, 0, -1)
+    mark(T.reset[:], "reset", 256, [[0, 64], [1, 4]], float(2 ** 28), 0, 0)
+    iota(T.ones[0:1, :], "ones", [[0, 128]], 1, 0)
+    iota(T.kc1[0:1, :], "kc1", [[16, 128], [0, 4]], 0, 0)
+    iota(T.kc2[0:1, :], "kc2", [[0, 64], [2048, 2], [4096, 2]], 0, 0)
+
+    off = T.lists
+    op("v", lambda: V.tensor_scalar(T.tmpf[:, 0:128], T.act32[:], 2048.0, icol, A.mult, A.add), reads=["act32", "icol"], writes=["t0"])
+    op("v", lambda: V.tensor_copy(T.nxu[:], T.nx32[:]), reads=["nx32"], writes=["nxu"])
+    op("v", lambda: V.tensor_tensor(T.tmpf[:, 128:256], T.tmpf[:, 0:128], T.mtile[:], A.add), reads=["t0", "mtile"], writes=["t1"])
+    op("v", lambda: V.tensor_scalar(cap16, cap, 0.0625, None, A.mult), reads=["cap"], writes=["cap16"])
+    op("v", lambda: V.tensor_copy(off[:, 0:128], T.tmpf[:, 128:256]), reads=["t1"], writes=["L0_0", "L0_1"])
+
+    rot = ("x0", "x1", "x2", "x3", "s0", "s1")
+    on_v = (2, 5, 7, 9, 11, 13, 15)
+    for i in range(16):
+        b = rot[i % 6]
+        op("p", lambda: P.matmul(T[b][:], T.bmat[:, 128 * i:128 * i + 128], T.nxh[:], True, True),
+           reads=["nxh", "bm%d" % i if i < 8 else "bm_hi"], banks=[b])
+        if i in on_v:
+            op("v", lambda: V.tensor_copy(T.nxrow[:, i:8192:16], T[b][:]), writes=[NXROW[i]], banks=[b])
+        else:
+            op("s", lambda: S.activation(T.nxrow[:, i:8192:16], T[b][:], F.Copy), writes=[NXROW[i]], banks=[b])
+    op("v", lambda: V.memset(T.sumrw[:], 0.0), writes=["sumrw%d" % j for j in range(4)])
+
+    def lst(k, lo, hi):
+        return off[:, 128 * k + lo:128 * k + hi]
+
+    def shadow(name, q, by_dma):
+        lo, hi = 512 * q, 512 * q + 512
+        if by_dma:
+            op("y", lambda: g.sync.dma_start(T.dc[:, lo:hi], T[name][:, lo:hi]), reads=K(name, lo, hi), writes=K("dc", lo, hi),
+               sem="sh%d" % q, inc=16)
+        else:
+            op("g", lambda: g.affine_select(T.dc[:, lo:hi], T[name][:, lo:hi], [[0, 512]], A.is_gt, 0.0, 1, 0),
+               reads=K(name, lo, hi), writes=K("dc", lo, hi))
+
+    def first(h):
+        lo, hi = 1024 * h, 1024 * h + 1024
+        op("v", lambda: V.tensor_scalar(T.ta[:, lo:hi], T.nxrow[:, 0:8192].indirect(lst(0, 64 * h, 64 * h + 64)), cj, 2048.0, A.add, A.max),
+           reads=NXROW + ["L0_%d" % h, "cj"], writes=K("ta", lo, hi))
+        for q in (2 * h, 2 * h + 1):
+            op("s", lambda: S.activation(T.da[:, 512 * q:512 * q + 512], T.rws[:, 0:8192].indirect(lst(0, 32 * q, 32 * q + 32)),
+                                         F.Identity, bias=cap16, scale=-1.0),
+               reads=["rws", "L0_%d" % h, "cap16"], writes=["da%d" % q])
+            shadow("da", q, q % 2 == 0)
+
+    def ext(name, h):
+        b = "e%d" % h
+
+        def fn():
+            for i in range(16):
+                ins = P.matmul(T[b][:, 0:64], T.zmat[:, 15 - i:143 - i], T[name][:, 1024 * h + i:1024 * h + 1024:16], i == 0, i == 15)
+            return ins
+        op("p", fn, reads=K(name, 1024 * h, 1024 * h + 1024) + ["zmat"], banks=[b])
+
+    def conv(k, h):
+        op("v", lambda: V.tensor_scalar(lst(k, 64 * h, 64 * h + 64), T["e%d" % h][:, 0:64], 2048.0, None, A.subtract),
+           writes=["L%d_%d" % (k, h)], banks=["e%d" % h])
+
+    def dstep(src, dst, k, q):
+        lo, hi = 512 * q, 512 * q + 512
+        op("v", lambda: V.tensor_tensor(T[dst][:, lo:hi], T[src][:, 0:2048].indirect(lst(k, 32 * q, 32 * q + 32)), T.dc[:, lo:hi], A.add),
+           reads=K(src, 0, 2048) + ["L%d_%d" % (k, q // 2), "dc%d" % q], writes=K(dst, lo, hi))
+
+    def tstep(src, dst, k, h):
+        lo, hi = 1024 * h, 1024 * h + 1024
+        op("s", lambda: S.activation(T[dst][:, lo:hi], T[src][:, 0:2048].indirect(lst(k, 64 * h, 64 * h + 64)), F.Copy),
+           reads=K(src, 0, 2048) + ["L%d_%d" % (k, h)], writes=K(dst, lo, hi))
+
+    sb = {(0, 0): "s0", (0, 1): "s1", (1, 0): "x0", (1, 1): "x1"}
+    pieces = [(h, a) for h in range(2) for a in range(3)]
+
+    def rwsum():
+        if not pieces:
+            return
+        h, a = pieces.pop(0)
+        b = sb[(h, a // 2)]
+        n = 64 if a < 2 else 32
+        p0 = 64 * (a % 2)
+        c0 = a * 2048 + 1024 * h
+
+        def fn():
+            for i in range(16):
+                ins = P.matmul(T[b][p0:p0 + n, i:128:16], T.rws[:, c0 + i:c0 + 16 * n:16], T.sel[:], True, True)
+            return ins
+        op("p", fn, reads=["rws", "sel"], banks=[b])
+
+    others = [T.cores[(rank + d) % N] for d in range(1, N)]
+    m = -1
+    for c in others:
+        m &= topo.mask(core, c)
+    neng = bin(m).count("1")
+    dsts = [DstId(rid=topo.addr(c)[0], pnc=topo.addr(c)[1]) for c in others]
+    narr = {}
+
+    def slot(r, h, k):
+        return ((r * 2 + h) * N + k) * 256
+
+    def send(r, h, lo, hi):
+        a = T.land[:, slot(r, h, rank) + lo:slot(r, h, rank) + hi]
+
+        def fn():
+            g.remote_dma_fused([RemoteDMATransfer(dst_ids=dsts, dma_engine_mask=m, remote_sem=T.sem["arr%d%d" % (r, h)],
+                                                  srcs=[a], dsts=[a] * (N - 1))], local_sem=T.sem.sent)
+        op("g", fn, reads=["own%d%d%d" % (r, h, p) for p in range(lo // 128, hi // 128)], sem="sent", inc=neng)
+        narr[(r, h)] = narr.get((r, h), 0) + neng * (N - 1)
+
+    def qv(h, a, lo, hi):
+        y0 = 4096 * h + 1024 * a
+        c0 = 2048 * a + 1024 * h
+        o = T.nxu[:, 128 * a + 64 * h + lo // 16:128 * a + 64 * h + hi // 16]
+        op("v", lambda: V.tensor_tensor(T.ybuf[:, y0 + lo:y0 + hi], T.da[:, 0:2048].indirect(o), T.rws[:, c0 + lo:c0 + hi], A.max),
+           reads=K("da", 0, 2048) + ["nxu", "rws"], writes=K("y", y0 + lo, y0 + hi))
+
+    SP = [(2, 512), (3, 0), (3, 512)]
+
+    def qg(h, j):
+        a, lo = SP[j]
+        g0 = 512 * (3 * h + j)
+        c0 = 2048 * a + 1024 * h + lo
+        oc = 128 * a + 64 * h + lo // 16
+        b = "x%d" % ((3 * h + j) % 4)
+        op("s", lambda: S.activation(T.gbuf[:, g0:g0 + 512], T.da[:, 0:2048].indirect(T.nxu[:, oc:oc + 32]), F.Copy),
+           reads=K("da", 0, 2048) + ["nxu"], writes=K("g", g0, g0 + 512))
+
+        def fn():
+            P.matmul(T[b][:], T.nident[:], T.rws[:, c0:c0 + 512], True, False)
+            return None
+        op("p", fn, reads=["rws", "nident"], banks=[b], inc=0)
+        op("p", lambda: P.matmul(T[b][:], T.ident[:], T.gbuf[:, g0:g0 + 512], False, True),
+           reads=K("g", g0, g0 + 512) + ["ident"], banks=[b])
+
+    def qr(h, j):
+        a, lo = SP[j]
+        y0 = 4096 * h + 1024 * a + lo
+        b = "x%d" % ((3 * h + j) % 4)
+        op("s", lambda: S.activation(T.ybuf[:, y0:y0 + 512], T[b][:], F.Relu), writes=K("y", y0, y0 + 512), banks=[b])
+
+    def qsum(h, p):
+        y0 = 4096 * h + 2048 * p
+        b = "s%d" % p
+
+        def fn():
+            for i in range(16):
+                ins = P.matmul(T[b][:, i:128:16], T.ybuf[:, y0 + i:y0 + 2048:16], T.sel[:], True, True)
+            return ins
+        op("p", fn, reads=K("y", y0, y0 + 2048) + ["sel"], banks=[b])
+
+    def qcv(r, h, p):
+        c0 = slot(r, h, rank) + 128 * p
+        j = 2 * h + p
+        op("v", lambda: V.tensor_tensor(T.land[:, c0:c0 + 128], T["s%d" % p][:, 0:128], T.sumrw[:, 128 * j:128 * j + 128], A.subtract),
+           reads=["sumrw%d" % j], writes=["own%d%d%d" % (r, h, p)], banks=["s%d" % p])
+
+    def keys(r, h):
+        b = "e%d" % h
+
+        def fn0():
+            P.matmul(T[b][:, 0:256], T.ones[0:1, :], T.kc1[0:1, 256 * h:256 * h + 256], True, False)
+            P.matmul(T[b][:, 0:256], T.ones[0:1, :], T.kc2[0:1, :], False, False)
+            for p in range(2):
+                c0 = slot(r, h, rank) + 128 * p
+                P.matmul(T[b][:, p:256:2], T.land[:, c0:c0 + 128], T.prm[:], False, False)
+            return None
+        op("p", fn0, reads=["ones", "kc1", "kc2", "prm", "own%d%d0" % (r, h), "own%d%d1" % (r, h)], banks=[b], inc=0)
+
+        def fn1():
+            ks = [k for k in range(N) if k != rank]
+            for k in ks:
+                for p in range(2):
+                    c0 = slot(r, h, k) + 128 * p
+                    ins = P.matmul(T[b][:, p:256:2], T.land[:, c0:c0 + 128], T.prm[:], False, k == ks[-1] and p == 1)
+            return ins
+        op("p", fn1, banks=[b], extra=[("arr%d%d" % (r, h), narr[(r, h)], "x", {})])
+
+    def choose(r, h):
+        b = "e%d" % h
+        sc = T.scan[:, 256 * h:256 * h + 256]
+        ki, km = T.ki[:, 64 * h:64 * h + 64], T.km[:, 64 * h:64 * h + 64]
+        op("v", lambda: V.tensor_tensor_scan(sc, T.reset[:], T[b][:, 0:256], 0.0, A.add, A.min),
+           reads=["reset"], writes=["sc%d" % h], banks=[b])
+        op("v", lambda: V.tensor_copy(ki, T.scan[:, 256 * h + 3:256 * h + 256:4]), reads=["sc%d" % h], writes=["ki%d" % h])
+        if r < RO - 1:
+            op("v", lambda: V.tensor_scalar(km, ki, 8191, None, A.bitwise_and), reads=["ki%d" % h], writes=["km%d" % h])
+            op("v", lambda: V.tensor_scalar(lst(0, 64 * h, 64 * h + 64), km, icol, None, A.add),
+               reads=["km%d" % h, "icol"], writes=["L0_%d" % h])
+        else:
+            op("v", lambda: V.tensor_scalar(km, ki, 11, 3, A.arith_shift_right, A.bitwise_and), reads=["ki%d" % h], writes=["km%d" % h])
+            op("v", lambda: V.tensor_copy(T.yas[:, 64 * h:64 * h + 64], km), reads=["km%d" % h], writes=["yas%d" % h])
+            op("y", lambda: g.sync.dma_start(T.ya[:, 64 * h:64 * h + 64], T.yas[:, 64 * h:64 * h + 64]),
+               reads=["yas%d" % h], sem="st", inc=16)
+
+    first(0)
+    first(1)
+    for r in range(RO):
+        ext("ta", 0)
+        conv(1, 0)
+        ext("ta", 1)
+        rwsum()
+        ds, ts = ["da", "db"], ["ta", "tb"]
+        for k in range(1, 4):
+            s0, s1 = ds[(k - 1) % 2], ds[k % 2]
+            t0, t1 = ts[(k - 1) % 2], ts[k % 2]
+            for h in range(2):
+                tstep(t0, t1, k, h)
+                for j in range(2):
+                    q = 2 * h + (j ^ (k % 2))
+                    dstep(s0, s1, k, q)
+                    if k < 3:
+                        shadow(s1, q, j == 0)
+                    elif q > 0:
+                        shadow(s1, q, False)
+                if h == 0:
+                    conv(k, 1)
+            ext(t1, 0)
+            rwsum()
+            conv(k + 1, 0)
+            ext(t1, 1)
+            if k < 3:
+                rwsum()
+        op("s", lambda: S.activation(T.gbuf[:, 3072:3584], T.db[:, 0:2048].indirect(lst(4, 0, 32)), F.Copy),
+           reads=K("db", 0, 2048) + ["L4_0"], writes=["g6"])
+
+        def fn():
+            P.matmul(T.x2[:], T.ident[:], T.db[:, 0:512], True, False)
+            return P.matmul(T.x2[:], T.ident[:], T.gbuf[:, 3072:3584], False, True)
+        op("p", fn, reads=["g6", "db0", "ident"], banks=["x2"])
+        dstep("db", "da", 4, 1)
+        conv(4, 1)
+        dstep("db", "da", 4, 3)
+        dstep("db", "da", 4, 2)
+        if r == 0:
+            for h in range(2):
+                for p in range(2):
+                    n = 128 if p == 0 else 32
+                    j = 2 * h + p
+                    op("s", lambda: S.activation(T.sumrw[0:n, 128 * j:128 * j + 128], T[sb[(h, p)]][0:n, 0:128], F.Copy),
+                       writes=["sumrw%d" % j], banks=[sb[(h, p)]])
+        op("s", lambda: S.activation(T.da[:, 0:512], T.x2[:], F.Copy), writes=["da0"], banks=["x2"])
+
+        for h in range(2):
+            if h == 0:
+                qv(h, 0, 0, 1024)
+            qg(h, 0)
+            qg(h, 1)
+            if h == 1:
+                qv(h, 0, 512, 1024)
+            qv(h, 1, 0, 1024)
+            qr(h, 0)
+            qg(h, 2)
+            qsum(h, 0)
+            qv(h, 2, 0, 512)
+            qr(h, 1)
+            qr(h, 2)
+            qsum(h, 1)
+            qcv(r, h, 0)
+            if h == 0:
+                if r == 0:
+                    send(r, h, 0, 128)
+                qv(1, 0, 0, 512)
+            qcv(r, h, 1)
+            if h == 0 and r == 0:
+                send(r, h, 128, 256)
+            else:
+                send(r, h, 0, 256)
+        if r == RO - 1:
+            for h in range(2):
+                op("s", lambda: S.activation(T.db[:, 1024 * h:1024 * h + 1024], T.da[:, 1024 * h:1024 * h + 1024], F.Relu),
+                   reads=K("da", 1024 * h, 1024 * h + 1024), writes=K("db", 1024 * h, 1024 * h + 1024))
+        for h in range(2):
+            keys(r, h)
+            choose(r, h)
+            if r < RO - 1:
+                first(h)
+            elif h == 0:
+                for j in range(2):
+                    lo, hi = 1024 * j, 1024 * j + 1024
+                    op("v", lambda: V.tensor_scalar(T.yrs[:, lo:hi], T.db[:, lo:hi], -1.0, cap, A.mult, A.add),
+                       reads=K("db", lo, hi) + ["cap"], writes=["yrs%d" % j])
+                    op("y", lambda: g.sync.dma_start(T.yr[:, lo:hi], T.yrs[:, lo:hi]), reads=["yrs%d" % j], sem="st", inc=16)
+
+    g.sync.wait_ge(T.sem.st, count["st"])
+    for s in ("cg", "sent", "cp", "cs", "cv"):
+        g.wait_ge(T.sem[s], count[s])

@@ -4,16 +4,33 @@ from concourse.mybir import AluOpType as A, ActivationFunctionType as F
 RO = 3
 BF, F32, I32, U16, F16 = "bfloat16", "float32", "int32", "uint16", "float16"
 SCRATCH = {n: ("sbuf", [128, w], d) for n, w, d in [
-    ("nx32", 512, I32), ("nxh", 512, F16), ("nxu", 512, U16), ("act32", 128, I32), ("capc", 4, F32), ("cols", 32, F32),
-    ("pint", 8, I32), ("rws", 8192, BF), ("nxrow", 8192, F32), ("ybuf", 8192, BF), ("gbuf", 3584, BF),
+    ("nx32", 512, I32), ("nxu", 512, U16), ("nxh", 512, F16), ("act32", 128, I32), ("capc", 4, F32), ("cols", 32, F32),
+    ("pint", 8, I32), ("rws", 8192, BF), ("nxrow", 8192, BF), ("ybuf", 8192, BF), ("gbuf", 3072, BF),
     ("ta", 2048, BF), ("tb", 2048, BF), ("da", 2048, BF), ("db", 2048, BF), ("dc", 2048, BF), ("yrs", 2048, BF),
-    ("lists", 640, U16), ("zeros", 1024, BF), ("bmat", 2048, BF), ("g16", 128, BF), ("colmat", 16, F32), ("xrow", 144, F32),
-    ("mtile", 128, F32), ("zmat", 144, BF), ("sel", 8, BF), ("ident", 128, BF), ("nident", 128, BF), ("prm", 128, BF),
-    ("reset", 256, BF), ("kc1", 512, BF), ("kc2", 256, BF), ("ones", 128, BF), ("sumrw", 512, F32), ("tmpf", 256, F32),
-    ("scan", 512, F32), ("ki", 128, I32), ("km", 128, I32), ("yas", 128, F32), ("land", RO * 2 * 4 * 256, F16)]}
-SCRATCH.update({n: ("psum", [128, 512], F32) for n in ("x0", "x1", "x2", "x3", "s0", "s1", "e0", "e1")})
-SEMAPHORES = ["cv", "cs", "cp", "cg", "ldnx", "ldrw", "ldact", "ldcap", "st", "sent", "sh0", "sh1", "sh2", "sh3"] + [
-    "arr%d%d" % (r, h) for r in range(RO) for h in range(2)]
+    ("l0", RO * 128, U16), ("lists", 512, U16), ("zeros", 512, BF), ("bmat", 2048, BF), ("g16", 128, BF), ("colmat", 16, F32),
+    ("xrow", 144, F32), ("mtile", 128, F32), ("zmat", 144, BF), ("sel", 8, BF), ("ident", 128, BF), ("nident", 128, BF),
+    ("prm", 256, BF), ("reset", 256, BF), ("kc1", 512, BF), ("kc2", 256, BF), ("ones", 128, BF), ("sumrw", 512, F32),
+    ("tmpf", 256, F32), ("nf", 640, BF), ("dnx", 640, F16), ("unx", 640, F16), ("scan", 512, F32), ("ki", 128, I32),
+    ("km", 128, I32), ("yas", 128, F32), ("land", RO * 16 * 128, F16)]}
+SCRATCH["xx"] = ("psum", [128, 2048], F32)
+SCRATCH.update({n: ("psum", [128, 512], F32) for n in ("s0", "s1", "e0", "e1")})
+NS = 512
+SOPS = [4, 4]
+ROWS_ON_V = (7, 9, 11, 13, 15)
+SHARED = 0
+QCV = [1, 0]
+ROWS = [8, 16]
+MODES = ["own", "own", "own"]
+AHEAD = True
+EARLY = 2
+R0PLAN = [("v", 0, False), ("v", 1, True), ("s", 2, True), ("v", 3, False)]
+R0S = 1
+SH0 = [True, False, False, False]
+CONV = [0, 0]
+YS = 256
+SEMAPHORES = ["cv", "cs", "cp", "cg", "ldnx", "ldrw", "ldact", "ldcap", "st", "sent"] + ["sh%d" % j for j in range(8)] + [
+    "%s%d%d" % (n, r, j) for n in ("far", "near", "chosen") for r in range(RO) for j in range(2)] + [
+    "act%d%d" % (r, k) for r in range(RO) for k in range(4)]
 
 
 def rank_program(g, core, T, topo):
@@ -71,17 +88,38 @@ def rank_program(g, core, T, topo):
             readers[k] = []
         return tok
 
-    def K(name, lo, hi):
-        return ["%s%d" % (name, j) for j in range(lo // 512, (hi + 511) // 512)]
+    def K(name, lo, hi, w=128):
+        return ["%s%d" % (name, j) for j in range(lo // w, (hi + w - 1) // w)]
 
     V, S, P = g.vector, g.scalar, g.tensor
-    icol, cj, zcol, cap16 = T.cols[:, 4:5], T.cols[:, 8:9], T.cols[:, 12:13], T.cols[:, 16:17]
+    icol, zcol, cap16, sgn, sgn16, pbias, tcol = [T.cols[:, 4 * j:4 * j + 1] for j in range(1, 8)]
     cap = T.capc[:, 0:1]
-    NXROW = ["nxrow%d" % i for i in range(16)]
+
+    mate0 = sorted(range(1, N), key=lambda k: not topo.same_plane(topo.chip(T.cores[0]), topo.chip(T.cores[k])))[0]
+    pairs = [[0, mate0], [k for k in range(1, N) if k != mate0]]
+    half = 0 if rank in pairs[0] else 1
+    pair, other = pairs[half], pairs[1 - half]
+    place = pair.index(rank)
+    partner, across = pair[1 - place], other[place]
+    others = [(rank + d) % N for d in range(1, N)]
+    QO, C, H = [], [], []
+
+    def orders(r):
+        first = 2 * half if MODES[r] == "pair" else 0
+        known_first = [first, first + 1, 2 - first, 3 - first]
+        QO[:] = known_first[2:] + known_first[:2] if MODES[r] == "pair" else known_first
+        C[:] = [512 * q for q in known_first]
+        H[:] = [C[0], C[2]]
+        if MODES[r] == "own":
+            mine = first = 2 * half + place
+            QO[:] = [2 - 2 * half, 3 - 2 * half, mine ^ 1, mine]
+            C[:] = [512 * q for q in (mine, mine ^ 1, mine ^ 2, mine ^ 3)]
+            H[:] = [1024 * half, 1024 - 1024 * half]
+    orders(0)
 
     op("y", lambda: g.sync.dma_start(T.nx32[:], T.nx[:]), writes=["nx32"], sem="ldnx", inc=16)
-    op("y", lambda: g.sync.dma_start(T.rws[:], T.rw[:]), writes=["rws"], sem="ldrw", inc=16)
     op("s", lambda: S.dma_start(T.act32[:], T.act0[:]), writes=["act32"], sem="ldact", inc=16)
+    op("y", lambda: g.sync.dma_start(T.rws[:], T.rw[:]), writes=["rws"], sem="ldrw", inc=16)
     op("s", lambda: S.dma_start(cap, T.cap[:]), writes=["cap"], sem="ldcap", inc=16)
 
     def iota(out, key, pattern, base, cm, flag=True):
@@ -94,306 +132,641 @@ def rank_program(g, core, T, topo):
         op("g", lambda: g.affine_select(out, T.zeros[:, 0:n], pattern, A.not_equal, fill, base, cm),
            reads=["zeros"], writes=[key])
 
-    op("v", lambda: V.memset(T.zeros[:], 0.0), writes=["zeros"])
+    def vts(out, in0, s1, s2, ops, reads, writes, banks=()):
+        op("v", lambda: V.tensor_scalar(out, in0, s1, s2, *ops), reads=reads, writes=writes, banks=banks)
+
+    def vcopy(out, in_, reads, writes):
+        op("v", lambda: V.tensor_copy(out, in_), reads=reads, writes=writes)
+
+    def vset(out, val, writes):
+        op("v", lambda: V.memset(out, val), writes=writes)
+
+    vset(T.zeros[:], 0.0, ["zeros"])
     iota(T.colmat[:], "colmat", [[-1, 16]], 0, 1)
     iota(T.g16[:], "g16", [[16, 8], [0, 16]], 0, 0)
     iota(T.pint[:, 0:1], "pint", [[0, 1]], 0, 1, False)
+    mark(T.bmat[:, 1024:1536], "bm_hi", 512, [[-1, 4], [-16, 8], [0, 16]], 1.0, -8, 1)
+    mark(T.bmat[:, 1536:2048], "bm_hj", 512, [[-1, 4], [-16, 8], [0, 16]], 1.0, -12, 1)
     iota(T.xrow[:], "xrow", [[1, 144]], 0, 0)
-    mark(T.bmat[:, 1024:2048], "bm_hi", 1024, [[-1, 8], [-16, 8], [0, 16]], 1.0, -8, 1)
     iota(T.mtile[:], "mtile", [[16, 128]], 0, 0)
+    vset(T.nf[:, 0:640:5], 0.0, ["nf0"])
+    vset(T.nf[:, 4:640:5], 1.0, ["nf4"])
+    vts(T.dnx[:, 0:640:5], T.zeros[:, 0:128], 0.0, None, [A.add], ["zeros"], ["dnx0"])
+    columns = [
+        lambda: vts(T.pint[:, 4:5], T.pint[:, 0:1], 15, None, [A.bitwise_and], ["pint"], ["pi"]),
+        lambda: vcopy(icol, T.pint[:, 4:5], ["pi"], ["icol"]),
+        lambda: vts(tcol, T.pint[:, 4:5], 8.0, 2.0, [A.is_ge, A.mult], ["pi"], ["tcol"]),
+        lambda: vts(sgn, tcol, -1.0, None, [A.add], ["tcol"], ["sgn"]),
+        lambda: vts(pbias, icol, -1031.5, sgn, [A.add, A.mult], ["icol", "sgn"], ["pb0"]),
+        lambda: vts(pbias, pbias, 3072.0, None, [A.add], ["pb0"], ["pbias"]),
+        lambda: vts(sgn16, sgn, 0.0625, None, [A.mult], ["sgn"], ["sgn16"]),
+        lambda: vts(zcol, T.colmat[:, 0:1], icol, 15.0, [A.subtract, A.add], ["colmat", "icol"], ["zcol"])]
     for i in range(8):
-        op("v", lambda: V.tensor_scalar(T.bmat[:, 128 * i:128 * i + 128], T.g16[:], T.colmat[:, i:i + 1], None, A.is_equal),
-           reads=["g16", "colmat"], writes=["bm%d" % i])
-    op("v", lambda: V.tensor_scalar(T.pint[:, 4:5], T.pint[:, 0:1], 15, None, A.bitwise_and), reads=["pint"], writes=["pi"])
-    op("v", lambda: V.tensor_copy(icol, T.pint[:, 4:5]), reads=["pi"], writes=["icol"])
-    op("v", lambda: V.tensor_scalar(cj, T.pint[:, 4:5], 2040.5, None, A.add), reads=["pi"], writes=["cj"])
-    op("v", lambda: V.tensor_scalar(zcol, T.colmat[:, 0:1], icol, 15.0, A.subtract, A.add), reads=["colmat", "icol"], writes=["zcol"])
-    op("v", lambda: V.tensor_scalar(T.zmat[:], T.xrow[:], zcol, 0.0625, A.is_equal, A.mult), reads=["xrow", "zcol"], writes=["zmat"])
-    op("v", lambda: V.tensor_scalar(T.sel[:], T.xrow[:, 15:128:16], zcol, None, A.is_equal), reads=["xrow", "zcol"], writes=["sel"])
-    op("v", lambda: V.tensor_copy(T.nxh[:], T.nx32[:]), reads=["nx32"], writes=["nxh"])
-    mark(T.ident[:], "ident", 128, [[-1, 128]], 1.0, 0, 1)
-    mark(T.nident[:], "nident", 128, [[-1, 128]], -1.0, 0, 1)
-    mark(T.prm[:], "prm", 128, [[1, 64], [64, 2]], 8192.0, 0, -1)
-    mark(T.reset[:], "reset", 256, [[0, 64], [1, 4]], float(2 ** 28), 0, 0)
-    iota(T.ones[0:1, :], "ones", [[0, 128]], 1, 0)
-    iota(T.kc1[0:1, :], "kc1", [[16, 128], [0, 4]], 0, 0)
-    iota(T.kc2[0:1, :], "kc2", [[0, 64], [2048, 2], [4096, 2]], 0, 0)
+        vts(T.bmat[:, 128 * i:128 * i + 128], T.g16[:], T.colmat[:, i:i + 1], None, [A.is_equal], ["g16", "colmat"], ["bm%d" % i])
+        if i % 2:
+            columns.pop(0)()
+    BM = ["bm_hi", "bm_hj"] + ["bm%d" % i for i in range(8)]
+    for a in range(1, 4):
+        vts(T.nf[:, a:640:5], T.act32[:], float(a), None, [A.is_lt], ["act32"], ["nf%d" % a])
+    vcopy(T.dnx[:, 4:640:5], T.nx32[:, 384:512], ["nx32"], ["dnx4"])
+    for a in range(1, 4):
+        op("v", lambda: V.tensor_tensor(T.dnx[:, a:640:5], T.nx32[:, 128 * a - 128:128 * a], T.nx32[:, 128 * a:128 * a + 128], A.subtract),
+           reads=["nx32"], writes=["dnx%d" % a])
+    columns.pop(0)()
+    op("v", lambda: V.tensor_tensor_scan(T.unx[:], T.dnx[:], T.nf[:], 0.0, A.add, A.mult),
+       reads=K("dnx", 0, 5, 1) + K("nf", 0, 5, 1), writes=["unx"])
+    while columns:
+        columns.pop(0)()
 
-    off = T.lists
-    op("v", lambda: V.tensor_scalar(T.tmpf[:, 0:128], T.act32[:], 2048.0, icol, A.mult, A.add), reads=["act32", "icol"], writes=["t0"])
-    op("v", lambda: V.tensor_copy(T.nxu[:], T.nx32[:]), reads=["nx32"], writes=["nxu"])
-    op("v", lambda: V.tensor_tensor(T.tmpf[:, 128:256], T.tmpf[:, 0:128], T.mtile[:], A.add), reads=["t0", "mtile"], writes=["t1"])
-    op("v", lambda: V.tensor_scalar(cap16, cap, 0.0625, None, A.mult), reads=["cap"], writes=["cap16"])
-    op("v", lambda: V.tensor_copy(off[:, 0:128], T.tmpf[:, 128:256]), reads=["t1"], writes=["L0_0", "L0_1"])
-
-    rot = ("x0", "x1", "x2", "x3", "s0", "s1")
-    on_v = (2, 5, 7, 9, 11, 13, 15)
-    for i in range(16):
-        b = rot[i % 6]
-        op("p", lambda: P.matmul(T[b][:], T.bmat[:, 128 * i:128 * i + 128], T.nxh[:], True, True),
-           reads=["nxh", "bm%d" % i if i < 8 else "bm_hi"], banks=[b])
-        if i in on_v:
-            op("v", lambda: V.tensor_copy(T.nxrow[:, i:8192:16], T[b][:]), writes=[NXROW[i]], banks=[b])
-        else:
-            op("s", lambda: S.activation(T.nxrow[:, i:8192:16], T[b][:], F.Copy), writes=[NXROW[i]], banks=[b])
-    op("v", lambda: V.memset(T.sumrw[:], 0.0), writes=["sumrw%d" % j for j in range(4)])
+    def lst0(r, lo, hi):
+        return T.l0[:, 128 * r + lo // 16:128 * r + hi // 16]
 
     def lst(k, lo, hi):
-        return off[:, 128 * k + lo:128 * k + hi]
+        return T.lists[:, 128 * (k - 1) + lo // 16:128 * (k - 1) + hi // 16]
 
-    def shadow(name, q, by_dma):
-        lo, hi = 512 * q, 512 * q + 512
+    def L(k, lo, hi):
+        return K("L%s_" % k, lo, hi, 512)
+
+    def X(b, lo=0, hi=512, step=1):
+        return T.xx[:, 512 * b + lo:512 * b + hi:step]
+
+    def pieces(e, out, b, writes):
+        if e == "v":
+            vts(out, X(b), sgn, pbias, [A.mult, A.add], ["sgn", "pbias"], writes, ["x%d" % b])
+        else:
+            op("s", lambda: S.activation(out, X(b), F.Identity, bias=pbias, scale=sgn), reads=["sgn", "pbias"], writes=writes, banks=["x%d" % b])
+
+    def trow_pe(q):
+        def fn():
+            for i in range(16):
+                ins = P.matmul(X(q, i, 512, 16), T.bmat[:, 128 * i:128 * i + 128], T.unx[:, 160 * q + 4:160 * q + 160:5], True, True)
+            return ins
+        op("p", fn, reads=["unx"] + BM, banks=["x%d" % q])
+
+    def trow_ev(q, e):
+        pieces(e, T.ta[:, 512 * q:512 * q + 512], q, K("ta", 512 * q, 512 * q + 512))
+
+    for q in range(4):
+        trow_pe(q)
+    vcopy(lst(1, 0, 2048), T.unx[:, 4:640:5], ["unx"], L(1, 0, 2048))
+    trow_ev(0, "s")
+    trow_ev(1, "s")
+    vts(T.tmpf[:, 0:128], T.act32[:], 2048.0, icol, [A.mult, A.add], ["act32", "icol"], ["t0"])
+    vts(T.zmat[:], T.xrow[:], zcol, sgn16, [A.is_equal, A.mult], ["xrow", "zcol", "sgn16"], ["zmat"])
+    op("v", lambda: V.tensor_tensor(T.tmpf[:, 128:256], T.tmpf[:, 0:128], T.mtile[:], A.add), reads=["t0", "mtile"], writes=["t1"])
+    vts(cap16, cap, 0.0625, None, [A.mult], ["cap"], ["cap16"])
+    trow_ev(2, "v")
+    trow_ev(3, "s")
+    vcopy(lst0(0, 0, 2048), T.tmpf[:, 128:256], ["t1"], L("a0", 0, 2048))
+    vcopy(T.nxh[:], T.nx32[:], ["nx32"], ["nxh"])
+    vts(T.sel[:], T.xrow[:, 15:128:16], zcol, None, [A.is_equal], ["xrow", "zcol"], ["sel"])
+    vcopy(T.nxu[:], T.nxh[:], ["nxh"], ["nxu"])
+    op("g", lambda: g.affine_select(T.sumrw[:], T.zeros[:], [[0, 512]], A.is_gt, 0.0, 1, 0), reads=["zeros"], writes=K("sumrw", 0, 4, 1))
+    mark(T.ident[:], "ident", 128, [[-1, 128]], 1.0, 0, 1)
+    mark(T.nident[:], "nident", 128, [[-1, 128]], -1.0, 0, 1)
+    mark(T.prm[:, 0:128], "prm0", 128, [[1, 32], [32, 4]], 512.0, 0, -1)
+    mark(T.prm[:, 128:256], "prm", 128, [[1, 32], [-32, 4]], 512.0, 96, -1)
+    if NS < 512:
+        vts(T.cols[:, 0:1], T.colmat[:, 0:1], 32.0 + NS // 16, None, [A.is_ge], ["colmat"], ["vmask"])
+    mark(T.reset[:], "reset", 256, [[0, 64], [1, 4]], float(2 ** 23), 0, 0)
+    iota(T.ones[0:1, :], "ones", [[0, 128]], 1, 0)
+    iota(T.kc1[0:1, :], "kc1", [[1, 128], [0, 4]], 0, 0)
+    iota(T.kc2[0:1, :], "kc2", [[0, 64], [128, 4]], 0, 0)
+
+    def shadow(name, lo, hi, by_dma):
         if by_dma:
             op("y", lambda: g.sync.dma_start(T.dc[:, lo:hi], T[name][:, lo:hi]), reads=K(name, lo, hi), writes=K("dc", lo, hi),
-               sem="sh%d" % q, inc=16)
+               sem="sh%d" % (lo // 256), inc=16)
         else:
-            op("g", lambda: g.affine_select(T.dc[:, lo:hi], T[name][:, lo:hi], [[0, 512]], A.is_gt, 0.0, 1, 0),
+            op("g", lambda: g.affine_select(T.dc[:, lo:hi], T[name][:, lo:hi], [[0, hi - lo]], A.is_gt, 0.0, 1, 0),
                reads=K(name, lo, hi), writes=K("dc", lo, hi))
 
-    def first(h):
-        lo, hi = 1024 * h, 1024 * h + 1024
-        op("v", lambda: V.tensor_scalar(T.ta[:, lo:hi], T.nxrow[:, 0:8192].indirect(lst(0, 64 * h, 64 * h + 64)), cj, 2048.0, A.add, A.max),
-           reads=NXROW + ["L0_%d" % h, "cj"], writes=K("ta", lo, hi))
-        for q in (2 * h, 2 * h + 1):
-            op("s", lambda: S.activation(T.da[:, 512 * q:512 * q + 512], T.rws[:, 0:8192].indirect(lst(0, 32 * q, 32 * q + 32)),
-                                         F.Identity, bias=cap16, scale=-1.0),
-               reads=["rws", "L0_%d" % h, "cap16"], writes=["da%d" % q])
-            shadow("da", q, q % 2 == 0)
+    def dfirst(e, r, lo, hi):
+        win = T.rws[:, 0:8192].indirect(lst0(r, lo, hi))
+        if e == "v":
+            vts(T.da[:, lo:hi], win, -1.0, cap16, [A.mult, A.add], ["rws", "cap16"] + L("a%d" % r, lo, hi), K("da", lo, hi))
+        else:
+            op("s", lambda: S.activation(T.da[:, lo:hi], win, F.Identity, bias=cap16, scale=-1.0),
+               reads=["rws", "cap16"] + L("a%d" % r, lo, hi), writes=K("da", lo, hi))
 
-    def ext(name, h):
-        b = "e%d" % h
+    def tfirst(r, lo, hi):
+        vcopy(T.ta[:, lo:hi], T.nxrow[:, 0:8192].indirect(lst0(r, lo, hi)), K("nxrow", 0, 16, 1) + L("a%d" % r, lo, hi), K("ta", lo, hi))
 
+    def ext(name, lo, hi, b):
         def fn():
             for i in range(16):
-                ins = P.matmul(T[b][:, 0:64], T.zmat[:, 15 - i:143 - i], T[name][:, 1024 * h + i:1024 * h + 1024:16], i == 0, i == 15)
+                ins = P.matmul(T[b][:, 0:(hi - lo) // 16], T.zmat[:, 15 - i:143 - i], T[name][:, lo + i:hi:16], i == 0, i == 15)
             return ins
-        op("p", fn, reads=K(name, 1024 * h, 1024 * h + 1024) + ["zmat"], banks=[b])
+        op("p", fn, reads=K(name, lo, hi) + ["zmat"], banks=[b])
 
-    def conv(k, h):
-        op("v", lambda: V.tensor_scalar(lst(k, 64 * h, 64 * h + 64), T["e%d" % h][:, 0:64], 2048.0, None, A.subtract),
-           writes=["L%d_%d" % (k, h)], banks=["e%d" % h])
+    def conv(k, lo, hi, b):
+        vts(lst(k, lo, hi), T[b][:, 0:(hi - lo) // 16], 1024.0, None, [A.add], [], L(k, lo, hi), [b])
 
-    def dstep(src, dst, k, q):
-        lo, hi = 512 * q, 512 * q + 512
-        op("v", lambda: V.tensor_tensor(T[dst][:, lo:hi], T[src][:, 0:2048].indirect(lst(k, 32 * q, 32 * q + 32)), T.dc[:, lo:hi], A.add),
-           reads=K(src, 0, 2048) + ["L%d_%d" % (k, q // 2), "dc%d" % q], writes=K(dst, lo, hi))
+    def exth(name, h):
+        ext(name, H[h], H[h] + 1024, "e%d" % h)
 
-    def tstep(src, dst, k, h):
-        lo, hi = 1024 * h, 1024 * h + 1024
-        op("s", lambda: S.activation(T[dst][:, lo:hi], T[src][:, 0:2048].indirect(lst(k, 64 * h, 64 * h + 64)), F.Copy),
-           reads=K(src, 0, 2048) + ["L%d_%d" % (k, h)], writes=K(dst, lo, hi))
+    def convh(k, h):
+        conv(k, H[h], H[h] + 1024, "e%d" % h)
 
-    sb = {(0, 0): "s0", (0, 1): "s1", (1, 0): "x0", (1, 1): "x1"}
-    pieces = [(h, a) for h in range(2) for a in range(3)]
+    def dstep(src, dst, k, lo, hi):
+        op("v", lambda: V.tensor_tensor(T[dst][:, lo:hi], T[src][:, 0:2048].indirect(lst(k, lo, hi)), T.dc[:, lo:hi], A.add),
+           reads=K(src, 0, 2048) + L(k, lo, hi) + K("dc", lo, hi), writes=K(dst, lo, hi))
 
-    def rwsum():
-        if not pieces:
-            return
-        h, a = pieces.pop(0)
-        b = sb[(h, a // 2)]
-        n = 64 if a < 2 else 32
-        p0 = 64 * (a % 2)
-        c0 = a * 2048 + 1024 * h
+    def dgather(src, k, lo, hi, j):
+        g0, n, b = 512 * j, hi - lo, "x%d" % j
 
         def fn():
-            for i in range(16):
-                ins = P.matmul(T[b][p0:p0 + n, i:128:16], T.rws[:, c0 + i:c0 + 16 * n:16], T.sel[:], True, True)
+            P.matmul(X(j, 0, n), T.ident[:], T[src][:, lo:hi], True, False)
+            return None
+        op("s", lambda: S.activation(T.gbuf[:, g0:g0 + n], T[src][:, 0:2048].indirect(lst(k, lo, hi)), F.Copy),
+           reads=K(src, 0, 2048) + L(k, lo, hi), writes=["g%d" % j])
+        op("p", fn, reads=K(src, lo, hi) + ["ident"], banks=[b], inc=0)
+        op("p", lambda: P.matmul(X(j, 0, n), T.ident[:], T.gbuf[:, g0:g0 + n], False, True), reads=K(src, lo, hi) + ["g%d" % j], banks=[b])
+
+    def dback(dst, lo, hi, j):
+        b = "x%d" % j
+        op("s", lambda: S.activation(T[dst][:, lo:hi], X(j, 0, hi - lo), F.Copy), writes=K(dst, lo, hi), banks=[b])
+
+    def tstep(e, src, dst, k, lo, hi):
+        win = T[src][:, 0:2048].indirect(lst(k, lo, hi))
+        op(e, (lambda: S.activation(T[dst][:, lo:hi], win, F.Copy)) if e == "s" else (lambda: V.tensor_copy(T[dst][:, lo:hi], win)),
+           reads=K(src, 0, 2048) + L(k, lo, hi), writes=K(dst, lo, hi))
+
+    def rwsum(j):
+        b = "s%d" % (j % 2)
+
+        def fn():
+            for a in range(2 if j % 2 and NS == 512 else 3):
+                c0, p0 = a * 2048 + 512 * QO[j], 32 * (3 - a if j % 2 else a)
+                for i in range(16):
+                    ins = P.matmul(T[b][p0:p0 + 32, i:128:16], T.rws[:, c0 + i:c0 + 512:16], T.sel[:], True, True)
             return ins
         op("p", fn, reads=["rws", "sel"], banks=[b])
 
-    others = [T.cores[(rank + d) % N] for d in range(1, N)]
-    m = -1
-    for c in others:
-        m &= topo.mask(core, c)
-    neng = bin(m).count("1")
-    dsts = [DstId(rid=topo.addr(c)[0], pnc=topo.addr(c)[1]) for c in others]
-    narr = {}
+    def rwback(j):
+        b = "s%d" % (j % 2)
+        lo, hi = (64, 128) if j % 2 else (0, 96)
+        op("v", lambda: V.tensor_copy(T.sumrw[lo:hi, 128 * j:128 * j + 128], T[b][lo:hi, 0:128]), writes=["sumrw%d" % j], banks=[b])
+        if j % 2 and NS < 512:
+            vts(T.sumrw[32:64, 128 * j:128 * j + 128], T[b][32:64, 0:128], T.cols[32:64, 0:1], None, [A.mult], ["vmask"], ["sumrw%d" % j], [b])
 
-    def slot(r, h, k):
-        return ((r * 2 + h) * N + k) * 256
+    def engines(ranks):
+        m = -1
+        for k in ranks:
+            m &= topo.mask(core, T.cores[k])
+        return m
 
-    def send(r, h, lo, hi):
-        a = T.land[:, slot(r, h, rank) + lo:slot(r, h, rank) + hi]
-
-        def fn():
-            g.remote_dma_fused([RemoteDMATransfer(dst_ids=dsts, dma_engine_mask=m, remote_sem=T.sem["arr%d%d" % (r, h)],
-                                                  srcs=[a], dsts=[a] * (N - 1))], local_sem=T.sem.sent)
-        op("g", fn, reads=["own%d%d%d" % (r, h, p) for p in range(lo // 128, hi // 128)], sem="sent", inc=neng)
-        narr[(r, h)] = narr.get((r, h), 0) + neng * (N - 1)
-
-    def qv(h, a, lo, hi):
-        y0 = 4096 * h + 1024 * a
-        c0 = 2048 * a + 1024 * h
-        o = T.nxu[:, 128 * a + 64 * h + lo // 16:128 * a + 64 * h + hi // 16]
-        op("v", lambda: V.tensor_tensor(T.ybuf[:, y0 + lo:y0 + hi], T.da[:, 0:2048].indirect(o), T.rws[:, c0 + lo:c0 + hi], A.max),
-           reads=K("da", 0, 2048) + ["nxu", "rws"], writes=K("y", y0 + lo, y0 + hi))
-
-    SP = [(2, 512), (3, 0), (3, 512)]
-
-    def qg(h, j):
-        a, lo = SP[j]
-        g0 = 512 * (3 * h + j)
-        c0 = 2048 * a + 1024 * h + lo
-        oc = 128 * a + 64 * h + lo // 16
-        b = "x%d" % ((3 * h + j) % 4)
-        op("s", lambda: S.activation(T.gbuf[:, g0:g0 + 512], T.da[:, 0:2048].indirect(T.nxu[:, oc:oc + 32]), F.Copy),
-           reads=K("da", 0, 2048) + ["nxu"], writes=K("g", g0, g0 + 512))
+    def write(ranks, src, dst, sem, reads, extra=()):
+        m = engines(ranks)
+        ids = [DstId(rid=topo.addr(T.cores[k])[0], pnc=topo.addr(T.cores[k])[1]) for k in ranks]
 
         def fn():
-            P.matmul(T[b][:], T.nident[:], T.rws[:, c0:c0 + 512], True, False)
+            g.remote_dma_fused([RemoteDMATransfer(dst_ids=ids, dma_engine_mask=m, remote_sem=T.sem[sem], srcs=[src], dsts=[dst] * len(ids))],
+                               local_sem=T.sem.sent)
+        return op("g", fn, reads=reads, extra=extra, sem="sent", inc=bin(m).count("1"))
+
+    def landed(name, k, ranks):
+        m = -1
+        for d in ranks:
+            m &= topo.mask(T.cores[k], T.cores[d])
+        return (name, bin(m).count("1"), "x", {})
+
+    def slot(r, j, n=1):
+        return T.land[:, (r * 16 + j) * 128:(r * 16 + j + n) * 128]
+
+    def qv(j, a):
+        lo = NS if a == 2 and j % 2 else 0
+        if lo == 512:
+            return
+        y0, c0, n = 2048 * j + 512 * (3 - a if j % 2 else a) + lo, 2048 * a + 512 * QO[j] + lo, 512 - lo
+        op("v", lambda: V.tensor_tensor(T.ybuf[:, y0:y0 + n], T.da[:, 0:2048].indirect(T.nxu[:, c0 // 16:(c0 + n) // 16]),
+                                        T.rws[:, c0:c0 + n], A.max),
+           reads=K("da", 0, 2048) + ["nxu", "rws"], writes=["yv%d%d" % (j, a)])
+
+    def spart(h, t):
+        c0 = 2048 * (3 if t < 2 else 2) + 512 * QO[2 * h + min(t, 1)]
+        return c0, 512 if t < 2 else NS, (3 * h + t) % 4
+
+    def qsub(h, t):
+        c0, n, b = spart(h, t)
+
+        def fn():
+            P.matmul(X(b, 0, n), T.nident[:], T.rws[:, c0:c0 + n], True, False)
             return None
-        op("p", fn, reads=["rws", "nident"], banks=[b], inc=0)
-        op("p", lambda: P.matmul(T[b][:], T.ident[:], T.gbuf[:, g0:g0 + 512], False, True),
-           reads=K("g", g0, g0 + 512) + ["ident"], banks=[b])
+        op("p", fn, reads=["rws", "nident"], banks=["x%d" % b], inc=0)
 
-    def qr(h, j):
-        a, lo = SP[j]
-        y0 = 4096 * h + 1024 * a + lo
-        b = "x%d" % ((3 * h + j) % 4)
-        op("s", lambda: S.activation(T.ybuf[:, y0:y0 + 512], T[b][:], F.Relu), writes=K("y", y0, y0 + 512), banks=[b])
+    def qg(h, t0, t1):
+        if t1 - t0 == 2 and QO[2 * h + 1] != QO[2 * h] + 1:
+            qg(h, t0, t0 + 1)
+            qg(h, t0 + 1, t1)
+            return
+        c0, g0 = spart(h, t0)[0], 512 * (3 * h + t0)
+        n = sum(spart(h, t)[1] for t in range(t0, t1))
+        op("s", lambda: S.activation(T.gbuf[:, g0:g0 + n], T.da[:, 0:2048].indirect(T.nxu[:, c0 // 16:(c0 + n) // 16]), F.Copy),
+           reads=K("da", 0, 2048) + ["nxu"], writes=K("g", 3 * h + t0, 3 * h + t1, 1))
+        for t in range(t0, t1):
+            c0, n, b = spart(h, t)
+            g0 = 512 * (3 * h + t)
+            op("p", lambda: P.matmul(X(b, 0, n), T.ident[:], T.gbuf[:, g0:g0 + n], False, True),
+               reads=["g%d" % (3 * h + t), "ident"], banks=["x%d" % b])
 
-    def qsum(h, p):
-        y0 = 4096 * h + 2048 * p
-        b = "s%d" % p
+    def qr(h, t0, t1):
+        y0, n = 4096 * h + 1536 + 512 * t0, sum(spart(h, t)[1] for t in range(t0, t1))
+        op("s", lambda: S.activation(T.ybuf[:, y0:y0 + n], X(spart(h, t0)[2], 0, n), F.Relu), writes=K("ys%d" % h, t0, t1, 1),
+           banks=["x%d" % spart(h, t)[2] for t in range(t0, t1)])
+
+    def qsum(j):
+        b = "s%d" % (j % 2)
 
         def fn():
             for i in range(16):
-                ins = P.matmul(T[b][:, i:128:16], T.ybuf[:, y0 + i:y0 + 2048:16], T.sel[:], True, True)
+                ins = P.matmul(T[b][:, i:128:16], T.ybuf[:, 2048 * j + i:2048 * j + 2048:16], T.sel[:], True, True)
             return ins
-        op("p", fn, reads=K("y", y0, y0 + 2048) + ["sel"], banks=[b])
+        op("p", fn, reads=["yv%d%d" % (j, a) for a in range(3)] + ["ys%d%d" % (j // 2, t) for t in ((1, 2) if j % 2 else (0,))] + ["sel"],
+           banks=[b])
 
-    def qcv(r, h, p):
-        c0 = slot(r, h, rank) + 128 * p
-        j = 2 * h + p
-        op("v", lambda: V.tensor_tensor(T.land[:, c0:c0 + 128], T["s%d" % p][:, 0:128], T.sumrw[:, 128 * j:128 * j + 128], A.subtract),
-           reads=["sumrw%d" % j], writes=["own%d%d%d" % (r, h, p)], banks=["s%d" % p])
-
-    def keys(r, h):
-        b = "e%d" % h
-
-        def fn0():
-            P.matmul(T[b][:, 0:256], T.ones[0:1, :], T.kc1[0:1, 256 * h:256 * h + 256], True, False)
-            P.matmul(T[b][:, 0:256], T.ones[0:1, :], T.kc2[0:1, :], False, False)
-            for p in range(2):
-                c0 = slot(r, h, rank) + 128 * p
-                P.matmul(T[b][:, p:256:2], T.land[:, c0:c0 + 128], T.prm[:], False, False)
-            return None
-        op("p", fn0, reads=["ones", "kc1", "kc2", "prm", "own%d%d0" % (r, h), "own%d%d1" % (r, h)], banks=[b], inc=0)
-
-        def fn1():
-            ks = [k for k in range(N) if k != rank]
-            for k in ks:
-                for p in range(2):
-                    c0 = slot(r, h, k) + 128 * p
-                    ins = P.matmul(T[b][:, p:256:2], T.land[:, c0:c0 + 128], T.prm[:], False, k == ks[-1] and p == 1)
-            return ins
-        op("p", fn1, banks=[b], extra=[("arr%d%d" % (r, h), narr[(r, h)], "x", {})])
-
-    def choose(r, h):
-        b = "e%d" % h
-        sc = T.scan[:, 256 * h:256 * h + 256]
-        ki, km = T.ki[:, 64 * h:64 * h + 64], T.km[:, 64 * h:64 * h + 64]
-        op("v", lambda: V.tensor_tensor_scan(sc, T.reset[:], T[b][:, 0:256], 0.0, A.add, A.min),
-           reads=["reset"], writes=["sc%d" % h], banks=[b])
-        op("v", lambda: V.tensor_copy(ki, T.scan[:, 256 * h + 3:256 * h + 256:4]), reads=["sc%d" % h], writes=["ki%d" % h])
-        if r < RO - 1:
-            op("v", lambda: V.tensor_scalar(km, ki, 8191, None, A.bitwise_and), reads=["ki%d" % h], writes=["km%d" % h])
-            op("v", lambda: V.tensor_scalar(lst(0, 64 * h, 64 * h + 64), km, icol, None, A.add),
-               reads=["km%d" % h, "icol"], writes=["L0_%d" % h])
+    def qcv(r, j):
+        b, c = "s%d" % (j % 2), j % 2
+        out = slot(r, 8 + j) if j < 2 else slot(r, 4 * c + 3 * place)
+        if MODES[r] == "all":
+            out = slot(r, 4 * rank + j)
+        if MODES[r] == "own":
+            out = slot(r, 8 + j)
+        op("v", lambda: V.tensor_tensor(out, T[b][:, 0:128], T.sumrw[:, 128 * j:128 * j + 128], A.subtract),
+           reads=["sumrw%d" % j], writes=["own%d%d" % (r, j)], banks=[b])
+        if MODES[r] == "own":
+            if j < 2:
+                write([other[j]], out, slot(r, place), "far%d%d" % (r, place), ["own%d%d" % (r, j)])
+            elif j == 2:
+                write([partner], out, slot(r, 2), "near%d0" % r, ["own%d%d" % (r, j)])
+        elif MODES[r] == "all":
+            if c == 1:
+                out = slot(r, 4 * rank + j - 1, 2)
+                write(others, out, out, "far%d%d" % (r, j // 2), ["own%d%d" % (r, j - 1), "own%d%d" % (r, j)])
+        elif j < 2:
+            write([other[j]], out, slot(r, 4 * j + 1 + place), "far%d%d" % (r, place), ["own%d%d" % (r, j)])
+        elif c == place:
+            out = slot(r, 4 * c + place, 3)
+            write([partner], out, out, "near%d%d" % (r, c), ["own%d%d" % (r, j)], far(r))
         else:
-            op("v", lambda: V.tensor_scalar(km, ki, 11, 3, A.arith_shift_right, A.bitwise_and), reads=["ki%d" % h], writes=["km%d" % h])
-            op("v", lambda: V.tensor_copy(T.yas[:, 64 * h:64 * h + 64], km), reads=["km%d" % h], writes=["yas%d" % h])
-            op("y", lambda: g.sync.dma_start(T.ya[:, 64 * h:64 * h + 64], T.yas[:, 64 * h:64 * h + 64]),
-               reads=["yas%d" % h], sem="st", inc=16)
+            write([partner], out, out, "near%d%d" % (r, c), ["own%d%d" % (r, j)])
 
-    first(0)
-    first(1)
-    for r in range(RO):
-        ext("ta", 0)
-        conv(1, 0)
-        ext("ta", 1)
-        rwsum()
-        ds, ts = ["da", "db"], ["ta", "tb"]
-        for k in range(1, 4):
-            s0, s1 = ds[(k - 1) % 2], ds[k % 2]
-            t0, t1 = ts[(k - 1) % 2], ts[k % 2]
-            for h in range(2):
-                tstep(t0, t1, k, h)
-                for j in range(2):
-                    q = 2 * h + (j ^ (k % 2))
-                    dstep(s0, s1, k, q)
-                    if k < 3:
-                        shadow(s1, q, j == 0)
-                    elif q > 0:
-                        shadow(s1, q, False)
-                if h == 0:
-                    conv(k, 1)
-            ext(t1, 0)
-            rwsum()
-            conv(k + 1, 0)
-            ext(t1, 1)
-            if k < 3:
-                rwsum()
-        op("s", lambda: S.activation(T.gbuf[:, 3072:3584], T.db[:, 0:2048].indirect(lst(4, 0, 32)), F.Copy),
-           reads=K("db", 0, 2048) + ["L4_0"], writes=["g6"])
+    def far(r):
+        return [landed("far%d%d" % (r, p), other[p], [rank]) for p in range(2)]
+
+    def keys(r, c, part):
+        b = "e%d" % c
+        out = T[b][:, 0:128]
+        here = [3 * place] + ([1, 2] if c == place else [])
+        todo = here if part == 0 else [j for j in range(4) if j not in here]
 
         def fn():
-            P.matmul(T.x2[:], T.ident[:], T.db[:, 0:512], True, False)
-            return P.matmul(T.x2[:], T.ident[:], T.gbuf[:, 3072:3584], False, True)
-        op("p", fn, reads=["g6", "db0", "ident"], banks=["x2"])
-        dstep("db", "da", 4, 1)
-        conv(4, 1)
-        dstep("db", "da", 4, 3)
-        dstep("db", "da", 4, 2)
-        if r == 0:
-            for h in range(2):
-                for p in range(2):
-                    n = 128 if p == 0 else 32
-                    j = 2 * h + p
-                    op("s", lambda: S.activation(T.sumrw[0:n, 128 * j:128 * j + 128], T[sb[(h, p)]][0:n, 0:128], F.Copy),
-                       writes=["sumrw%d" % j], banks=[sb[(h, p)]])
-        op("s", lambda: S.activation(T.da[:, 0:512], T.x2[:], F.Copy), writes=["da0"], banks=["x2"])
+            if part == 0:
+                P.matmul(out, T.ones[0:1, :], T.kc1[0:1, C[c] // 4:C[c] // 4 + 128], True, False)
+                P.matmul(out, T.ones[0:1, :], T.kc2[0:1, 0:128], False, False)
+            for j in todo:
+                ins = P.matmul(out, slot(r, 4 * c + j), T.prm[:, 128 * c:128 * c + 128], False, part == 1 and j == todo[-1])
+            return ins if part else None
+        if part == 0:
+            op("p", fn, reads=["ones", "kc1", "kc2", "prm", "own%d%d" % (r, 2 + c)], banks=[b], extra=far(r) if c == place else [], inc=0)
+        else:
+            op("p", fn, banks=[b], extra=[landed("near%d%d" % (r, c), partner, [rank])])
 
-        for h in range(2):
-            if h == 0:
-                qv(h, 0, 0, 1024)
-            qg(h, 0)
-            qg(h, 1)
-            if h == 1:
-                qv(h, 0, 512, 1024)
-            qv(h, 1, 0, 1024)
-            qr(h, 0)
-            qg(h, 2)
-            qsum(h, 0)
-            qv(h, 2, 0, 512)
-            qr(h, 1)
-            qr(h, 2)
-            qsum(h, 1)
-            qcv(r, h, 0)
-            if h == 0:
-                if r == 0:
-                    send(r, h, 0, 128)
-                qv(1, 0, 0, 512)
-            qcv(r, h, 1)
-            if h == 0 and r == 0:
-                send(r, h, 128, 256)
-            else:
-                send(r, h, 0, 256)
-        if r == RO - 1:
-            for h in range(2):
-                op("s", lambda: S.activation(T.db[:, 1024 * h:1024 * h + 1024], T.da[:, 1024 * h:1024 * h + 1024], F.Relu),
-                   reads=K("da", 1024 * h, 1024 * h + 1024), writes=K("db", 1024 * h, 1024 * h + 1024))
-        for h in range(2):
-            keys(r, h)
-            choose(r, h)
-            if r < RO - 1:
-                first(h)
-            elif h == 0:
+    def keys_own(r, part):
+        out = T.e0[:, 0:128]
+
+        def fn():
+            if part == 0:
+                P.matmul(out, T.ones[0:1, :], T.kc1[0:1, C[0] // 4:C[0] // 4 + 128], True, False)
+                P.matmul(out, T.ones[0:1, :], T.kc2[0:1, 0:128], False, False)
                 for j in range(2):
-                    lo, hi = 1024 * j, 1024 * j + 1024
-                    op("v", lambda: V.tensor_scalar(T.yrs[:, lo:hi], T.db[:, lo:hi], -1.0, cap, A.mult, A.add),
-                       reads=K("db", lo, hi) + ["cap"], writes=["yrs%d" % j])
-                    op("y", lambda: g.sync.dma_start(T.yr[:, lo:hi], T.yrs[:, lo:hi]), reads=["yrs%d" % j], sem="st", inc=16)
+                    P.matmul(out, slot(r, j), T.prm[:, 128 * place:128 * place + 128], False, False)
+            elif part == 1:
+                P.matmul(out, slot(r, 11), T.prm[:, 128:256], False, False)
+            else:
+                return P.matmul(out, slot(r, 2), T.prm[:, 0:128], False, True)
+            return None
+        op("p", fn, reads=["ones", "kc1", "kc2", "prm"] + (["own%d3" % r] if part == 1 else []), banks=["e0"],
+           extra=[far(r), [], [landed("near%d0" % r, partner, [rank])]][part], inc=part // 2)
+
+    def choose(r, c):
+        b, lo, hi = "e%d" % c, C[c], C[c] + 512
+        if MODES[r] == "own":
+            rest = [partner, across, other[1 - place]]
+            sc, ki, km = T.scan[:, 0:128], T.ki[:, 0:32], T.km[:, 0:32]
+            op("v", lambda: V.tensor_tensor_scan(sc, T.reset[:, 0:128], T[b][:, 0:128], 0.0, A.add, A.min), reads=["reset"], writes=["scan0"], banks=[b])
+            vcopy(ki, T.scan[:, 3:128:4], ["scan0"], ["ki0"])
+            if r < RO - 1:
+                out, key = lst0(r + 1, lo, hi), L("a%d" % (r + 1), lo, hi)
+                vts(km, ki, 511, None, [A.bitwise_and], ["ki0"], ["km0"])
+                vts(out, km, 16.0, icol, [A.mult, A.add], ["km0", "icol"], key)
+            else:
+                out, key = T.yas[:, lo // 16:hi // 16], ["yas0"]
+                vts(km, ki, 7, 3, [A.arith_shift_right, A.bitwise_and], ["ki0"], ["km0"])
+                vcopy(out, km, ["km0"], key)
+            write(rest, out, out, "act%d%d" % (r, rank), key)
+            for j in range(1, 4):
+                for name in (L("a%d" % (r + 1), C[j], C[j] + 512) if r < RO - 1 else ["yas%d" % j]):
+                    lastw[name] = landed("act%d%d" % (r, rest[j - 1]), rest[j - 1], [k for k in range(N) if k != rest[j - 1]])
+            return
+        sc, ki, km = T.scan[:, 128 * c:128 * c + 128], T.ki[:, 32 * c:32 * c + 32], T.km[:, 32 * c:32 * c + 32]
+        op("v", lambda: V.tensor_tensor_scan(sc, T.reset[:, 0:128], T[b][:, 0:128], 0.0, A.add, A.min), reads=["reset"], writes=["scan%d" % c], banks=[b])
+        vcopy(ki, T.scan[:, 128 * c + 3:128 * c + 128:4], ["scan%d" % c], ["ki%d" % c])
+        if r < RO - 1:
+            out, key = lst0(r + 1, lo, hi), L("a%d" % (r + 1), lo, hi)
+            vts(km, ki, 511, None, [A.bitwise_and], ["ki%d" % c], ["km%d" % c])
+            vts(out, km, 16.0, icol, [A.mult, A.add], ["km%d" % c, "icol"], key)
+            write([across], out, out, "chosen%d%d" % (r, c), key)
+            for name in L("a%d" % (r + 1), C[2 + c], C[2 + c] + 512):
+                lastw[name] = landed("chosen%d%d" % (r, c), across, [rank])
+        else:
+            vts(km, ki, 7, 3, [A.arith_shift_right, A.bitwise_and], ["ki%d" % c], ["km%d" % c])
+            vcopy(T.yas[:, lo // 16:hi // 16], km, ["km%d" % c], ["yas%d" % c])
+            if c == 1:
+                out = T.yas[:, H[0] // 16:H[0] // 16 + 64]
+                write([across], out, out, "chosen%d%d" % (r, c), ["yas0", "yas1"])
+                lastw["yas2"] = landed("chosen%d%d" % (r, c), across, [rank])
+
+    def keys_all(r, h, part):
+        b = "e%d" % h
+        todo = [(k, q) for k in ([rank] if part == 0 else others) for q in range(2)]
+
+        def fn():
+            if part == 0:
+                P.matmul(T[b][:, 0:256], T.ones[0:1, :], T.kc1[0:1, 256 * h:256 * h + 256], True, False)
+                P.matmul(T[b][:, 0:256], T.ones[0:1, :], T.kc2[0:1, :], False, False)
+            for k, q in todo:
+                ins = P.matmul(T[b][:, 128 * q:128 * q + 128], slot(r, 4 * k + 2 * h + q), T.prm[:, 128 * q:128 * q + 128], False,
+                               part == 1 and (k, q) == todo[-1])
+            return ins if part else None
+        if part == 0:
+            op("p", fn, reads=["ones", "kc1", "kc2", "prm", "own%d%d" % (r, 2 * h), "own%d%d" % (r, 2 * h + 1)], banks=[b], inc=0)
+        else:
+            a = landed("far%d%d" % (r, h), others[0], [rank])
+            op("p", fn, banks=[b], extra=[(a[0], a[1] * (N - 1), "x", {})])
+
+    def choose_all(r, c):
+        b, lo, hi = "e%d" % c, 1024 * c, 1024 * c + 1024
+        sc, ki, km = T.scan[:, 256 * c:256 * c + 256], T.ki[:, 64 * c:64 * c + 64], T.km[:, 64 * c:64 * c + 64]
+        op("v", lambda: V.tensor_tensor_scan(sc, T.reset[:], T[b][:, 0:256], 0.0, A.add, A.min), reads=["reset"], writes=["scan%d" % c], banks=[b])
+        vcopy(ki, T.scan[:, 256 * c + 3:256 * c + 256:4], ["scan%d" % c], ["ki%d" % c])
+        if r < RO - 1:
+            out, key = lst0(r + 1, lo, hi), L("a%d" % (r + 1), lo, hi)
+            vts(km, ki, 511, None, [A.bitwise_and], ["ki%d" % c], ["km%d" % c])
+            vts(out, km, 16.0, icol, [A.mult, A.add], ["km%d" % c, "icol"], key)
+        else:
+            vts(km, ki, 7, 3, [A.arith_shift_right, A.bitwise_and], ["ki%d" % c], ["km%d" % c])
+            vcopy(T.yas[:, lo // 16:hi // 16], km, ["km%d" % c], ["yas%d" % c])
+
+    def rows_pe(i):
+        b = (i + 2 - EARLY) % 4
+        op("p", lambda: P.matmul(X(b), T.bmat[:, 128 * i:128 * i + 128], T.nxh[:], True, True), reads=["nxh"] + BM, banks=["x%d" % b])
+
+    def rows_ev(i):
+        pieces("v" if i in ROWS_ON_V else "s", T.nxrow[:, i:8192:16], (i + 2 - EARLY) % 4, ["nxrow%d" % i])
+
+    ds, ts = ["da", "db"], ["ta", "tb"]
+
+    def helped(k, small_first, pending=None, last=True):
+        s0, s1 = ds[(k - 1) % 2], ds[k % 2]
+        y, z = (C[3] + 256, C[3]) if k % 2 == 0 else (C[3], C[3] + 256)
+        parts = [(C[0], C[0] + 512, 2 * (k % 2)), (y, y + 256, 2 * (k % 2) + 1)]
+        if last and not small_first and YS < 256:
+            dgather(s0, k, *parts[0])
+            dstep(s0, s1, k, C[1], C[1] + 512)
+            pending()
+            if YS:
+                dgather(s0, k, C[3] + 512 - YS, C[3] + 512, parts[1][2])
+            dback(s1, *parts[0])
+            dstep(s0, s1, k, C[2], C[2] + 512)
+            dstep(s0, s1, k, C[3], C[3] + 512 - YS)
+            if YS:
+                dback(s1, C[3] + 512 - YS, C[3] + 512, parts[1][2])
+            return
+        if small_first:
+            parts.reverse()
+        dgather(s0, k, *parts[0])
+        dstep(s0, s1, k, C[1], C[1] + 512)
+        if not last:
+            shadow(s1, C[1], C[1] + 512, False)
+        if pending:
+            pending()
+        dgather(s0, k, *parts[1])
+        dback(s1, *parts[0])
+        if small_first and not last:
+            shadow(s1, y, y + 256, True)
+        dstep(s0, s1, k, C[2], C[2] + 512)
+        if not last:
+            shadow(s1, C[2], C[2] + 512, False)
+        dstep(s0, s1, k, z, z + 256)
+        dback(s1, *parts[1])
+        if not small_first and not last:
+            shadow(s1, y, y + 256, True)
+
+    def beside(k, kt, kh, early=None):
+        s0, s1 = ds[(k - 1) % 2], ds[k % 2]
+        t0, t1 = ts[(kt - 1) % 2], ts[kt % 2]
+        order = (1, 0, 2, 3) if (kh - k) % 2 else (0, 1, 3, 2)
+        z = C[3] + 256 * (kh % 2)
+        for h in range(2):
+            tstep("s", t0, t1, kt, H[h], H[h] + 1024)
+            for p in range(2):
+                j = order[2 * h + p]
+                if k == 0:
+                    dfirst("s" if R0S and (h, p) == (0, 1) else "v", 0, C[j], C[j] + 512)
+                else:
+                    dstep(s0, s1, k, C[j], C[j] + 512)
+                if k + 1 < kh:
+                    shadow(s1, C[j], C[j] + 512, p == 0)
+                elif j in (1, 2):
+                    shadow(s1, C[j], C[j] + 512, j == 1)
+                elif j == 3:
+                    shadow(s1, z, z + (512 - YS if kh == 4 else 256), False)
+                if h == 0 and p == CONV[0]:
+                    (early or (lambda: convh(kt, 1)))()
+                if h == 1 and p == (CONV[1] if k else 1):
+                    convh(kt + 1, 0)
+            exth(t1, h)
+            if k + h > 0:
+                rwnext()
+
+    def rwnext():
+        if sums:
+            j = sums.pop(0)
+            if j > 1:
+                rwback(j - 2)
+            if j < 4:
+                rwsum(j)
+
+    sums = list(range(6))
+    for k in range(1, SHARED + 1):
+        t0, t1 = ts[(k - 1) % 2], ts[k % 2]
+        tstep("v", t0, t1, k, C[0], C[0] + 512)
+        tstep("s", t0, t1, k, C[1], C[1] + 512)
+        if k > 1:
+            convh(k, 1)
+        exth(t1, 0)
+        tstep("v", t0, t1, k, C[2], C[2] + 512)
+        tstep("s", t0, t1, k, C[3], C[3] + 512)
+        convh(k + 1, 0)
+        exth(t1, 1)
+    kh = 3 - SHARED
+    if AHEAD:
+        for h in range(2):
+            tstep("s", "ta", "tb", 1, H[h], H[h] + 1024)
+            exth("tb", h)
+        for e, j, by_dma in R0PLAN:
+            dfirst(e, 0, C[j], C[j] + 512)
+            shadow("da", C[j], C[j] + 512, by_dma)
+        convh(2, 0)
+        rwnext()
+        beside(1, 2, 3)
+        for i in range(EARLY):
+            rows_pe(i)
+        beside(2, 3, 3)
+        for i in range(EARLY):
+            rows_ev(i)
+    for k in range(0 if AHEAD else kh):
+        if k == 0:
+            if SHARED:
+                convh(SHARED + 1, 1)
+            beside(k, SHARED + 1 + k, kh, lambda: None)
+        else:
+            beside(k, SHARED + 1 + k, kh)
+    for k in range(kh, 5):
+        helped(k, k < 4, (lambda: convh(4, 1)) if k == kh else (lambda: None), k == 4)
+        rwnext()
+    while sums:
+        rwnext()
+
+    for r in range(RO):
+        if r > 0:
+            beside(1, 1, 4)
+            beside(2, 2, 4)
+            beside(3, 3, 4)
+            helped(4, False, lambda: convh(4, 1))
+        orders(r)
+
+        for h, t in ((0, 0), (0, 1), (0, 2), (1, 0)):
+            qsub(h, t)
+        for h in range(2):
+            j = 2 * h
+            qv(j, 0)
+            if h == 1:
+                qsum(1)
+                qcv(r, 1)
+            if SOPS[h] == 4:
+                qg(h, 0, 2)
+                qg(h, 2, 3)
+                qr(h, 0, 1)
+            else:
+                qg(h, 0, 1)
+                qg(h, 1, 2)
+                qr(h, 0, 1)
+            qv(j, 1)
+            qv(j, 2)
+            if h == 0:
+                qsub(1, 1)
+            qsum(j)
+            if SOPS[h] > 4:
+                qg(h, 2, 3)
+            qv(j + 1, 1)
+            if QCV[h] == 0:
+                qcv(r, j)
+            qv(j + 1, 0)
+            if QCV[h] == 1:
+                qcv(r, j)
+            qv(j + 1, 2)
+            if h == 1 and r == 0:
+                rows_pe(EARLY)
+                rows_pe(EARLY + 1)
+            if SOPS[h] < 6:
+                qr(h, 1, 3)
+            else:
+                qr(h, 1, 2)
+                qr(h, 2, 3)
+            if h == 0:
+                qsub(1, 2)
+        qsum(3)
+        if r == 0:
+            rows_ev(EARLY)
+            rows_ev(EARLY + 1)
+            for i in range(EARLY + 2, EARLY + 4):
+                rows_pe(i)
+                rows_ev(i)
+        if r == RO - 1:
+            vts(T.db[:, 1024:2048], T.da[:, 1024:2048], 0.0, -1.0, [A.max, A.mult], K("da", 1024, 2048), K("db", 1024, 2048))
+            op("s", lambda: S.activation(T.db[:, 0:1024], T.da[:, 0:1024], F.Relu), reads=K("da", 0, 1024), writes=K("db", 0, 1024))
+            op("s", lambda: S.activation(T.yrs[:, 1024:2048], T.db[:, 1024:2048], F.Identity, bias=cap),
+               reads=K("db", 1024, 2048) + ["cap"], writes=["yrs1"])
+        qcv(r, 3)
+        if r == RO - 1:
+            vts(T.yrs[:, 0:1024], T.db[:, 0:1024], -1.0, cap, [A.mult, A.add], K("db", 0, 1024) + ["cap"], ["yrs0"])
+            for h in range(2):
+                op("y", lambda: g.sync.dma_start(T.yr[:, 1024 * h:1024 * h + 1024], T.yrs[:, 1024 * h:1024 * h + 1024]),
+                   reads=["yrs%d" % h], sem="st", inc=16)
+
+        def rows(lo, hi):
+            for i in range(max(lo, EARLY + 4), hi if r == 0 else lo):
+                rows_pe(i)
+                rows_ev(i)
+
+        def start(j):
+            lo, hi = C[j], C[j] + 512
+            tfirst(r + 1, lo, hi)
+            dfirst("s", r + 1, lo, hi)
+            shadow("da", lo, hi, SH0[j])
+
+        if MODES[r] == "all":
+            rows(4, 16)
+            keys_all(r, 0, 0)
+            keys_all(r, 0, 1)
+            keys_all(r, 1, 0)
+            choose_all(r, 0)
+            if r < RO - 1:
+                start(0)
+                start(1)
+                ext("ta", 0, 1024, "e0")
+            keys_all(r, 1, 1)
+            if r < RO - 1:
+                conv(1, 0, 1024, "e0")
+            choose_all(r, 1)
+            if r < RO - 1:
+                tfirst(r + 1, 1024, 2048)
+                for lo in (1024, 1536):
+                    dfirst("s", r + 1, lo, lo + 512)
+                    shadow("da", lo, lo + 512, False)
+                ext("ta", 1024, 2048, "e1")
+            else:
+                op("s", lambda: S.dma_start(T.ya[:], T.yas[:]), reads=["yas0", "yas1"], sem="st", inc=16)
+            continue
+        if MODES[r] == "own":
+            keys_own(r, 0)
+            keys_own(r, 1)
+            rows(4, ROWS[0])
+            keys_own(r, 2)
+            choose(r, 0)
+            rows(ROWS[0], 16)
+        else:
+            rows(4, ROWS[0])
+            keys(r, 0, 0)
+            keys(r, 0, 1)
+            keys(r, 1, 0)
+            choose(r, 0)
+            rows(ROWS[0], ROWS[1])
+            keys(r, 1, 1)
+            choose(r, 1)
+            rows(ROWS[1], 16)
+        if r < RO - 1:
+            start(0)
+            start(1)
+            ext("ta", H[0], H[0] + 1024, "e0")
+            start(2)
+            conv(1, H[0], H[0] + 1024, "e0")
+            start(3)
+            exth("ta", 1)
+        else:
+            op("s", lambda: S.dma_start(T.ya[:], T.yas[:]), reads=["yas0", "yas1", "yas2", "yas3"], sem="st", inc=16)
 
     g.sync.wait_ge(T.sem.st, count["st"])
     for s in ("cg", "sent", "cp", "cs", "cv"):

from concourse.bass import DstId, RemoteDMATransfer
from concourse.mybir import AluOpType as A, ActivationFunctionType as F

RO = 3
BF, F32, I32, U16, F16 = "bfloat16", "float32", "int32", "uint16", "float16"
SCRATCH = {n: ("sbuf", [128, w], d) for n, w, d in [
    ("nx32", 512, I32), ("nxu", 512, U16), ("nxh", 512, F16), ("act32", 128, I32), ("capc", 4, F32), ("cols", 32, F32),
    ("pint", 8, I32), ("rws", 8192, BF), ("nxrow", 8192, BF), ("ybuf", 8192, BF), ("gbuf", 3072, BF),
    ("ta", 2048, BF), ("tb", 2048, BF), ("da", 2048, BF), ("db", 2048, BF), ("dc", 2048, BF), ("yrs", 2048, BF),
    ("l0", RO * 128, U16), ("lists", 512, U16), ("zeros", 512, BF), ("bmat", 2048, BF), ("g16", 128, BF), ("colmat", 16, F32),
    ("xrow", 144, F32), ("mtile", 128, F32), ("zmat", 144, BF), ("sel", 8, BF), ("ident", 128, BF), ("nident", 128, BF),
    ("prm", 256, BF), ("reset", 256, BF), ("kc1", 512, BF), ("kc2", 256, BF), ("ones", 128, BF), ("sumrw", 512, F32),
    ("tmpf", 256, F32), ("nf", 640, BF), ("dnx", 640, F16), ("unx", 640, F16), ("scan", 512, F32), ("ki", 128, I32),
    ("km", 128, I32), ("yas", 128, F32), ("land", RO * 16 * 128, F16)]}
SCRATCH["xx"] = ("psum", [128, 2048], F32)
SCRATCH.update({n: ("psum", [128, 512], F32) for n in ("s0", "s1", "e0", "e1")})
NS = 512
SOPS = [4, 4]
ROWS_ON_V = (7, 9, 11, 13, 15)
SHARED = 0
QCV = [1, 0]
ROWS = [8, 16]
MODES = ["own", "own", "own"]
AHEAD = True
EARLY = 2
R0PLAN = [("v", 0, False), ("v", 1, True), ("s", 2, True), ("v", 3, False)]
R0S = 1
SH0 = [True, False, False, False]
CONV = [0, 0]
YS = 256
SEMAPHORES = ["cv", "cs", "cp", "cg", "ldnx", "ldrw", "ldact", "ldcap", "st", "sent"] + ["sh%d" % j for j in range(8)] + [
    "%s%d%d" % (n, r, j) for n in ("far", "near", "chosen") for r in range(RO) for j in range(2)] + [
    "act%d%d" % (r, k) for r in range(RO) for k in range(4)]


def rank_program(g, core, T, topo):
    rank = T.rank_of(core)
    if rank is None:
        return
    N = len(T.cores)
    Q = {"g": g, "v": g.vector, "s": g.scalar, "p": g.tensor, "y": g.sync}
    CS = {"g": "cg", "v": "cv", "s": "cs", "p": "cp"}
    count = {}
    known = {e: {} for e in Q}
    lastw = {}
    readers = {}

    def wait(e, tok):
        sem, val, clock = tok[0], tok[1], tok[3]
        if known[e].get(sem, 0) >= val:
            return
        Q[e].wait_ge(T.sem[sem], val)
        known[e][sem] = val
        for k, v in clock.items():
            if known[e].get(k, 0) < v:
                known[e][k] = v

    def op(e, fn, reads=(), writes=(), banks=(), extra=(), sem=None, inc=1):
        deps = list(extra)
        for k in reads:
            if k in lastw:
                deps.append(lastw[k])
        for k in writes:
            if k in lastw:
                deps.append(lastw[k])
            deps.extend(readers.get(k, []))
        for k in banks:
            if k in lastw and lastw[k][2] != e:
                deps.append(lastw[k])
        best = {}
        for t in deps:
            if e == "p" and t[2] == "p":
                continue
            if t[0] not in best or best[t[0]][1] < t[1]:
                best[t[0]] = t
        for t in sorted(best.values(), key=lambda t: -len(t[3])):
            wait(e, t)
        ins = fn()
        s = sem or CS[e]
        count[s] = count.get(s, 0) + inc
        if ins is not None:
            ins.then_inc(T.sem[s], inc)
        tok = (s, count[s], e, dict(known[e]))
        for k in reads:
            readers.setdefault(k, []).append(tok)
        for k in list(writes) + list(banks):
            lastw[k] = tok
            readers[k] = []
        return tok

    def K(name, lo, hi, w=128):
        return ["%s%d" % (name, j) for j in range(lo // w, (hi + w - 1) // w)]

    V, S, P = g.vector, g.scalar, g.tensor
    icol, zcol, cap16, sgn, sgn16, pbias, tcol = [T.cols[:, 4 * j:4 * j + 1] for j in range(1, 8)]
    cap = T.capc[:, 0:1]

    mate0 = sorted(range(1, N), key=lambda k: not topo.same_plane(topo.chip(T.cores[0]), topo.chip(T.cores[k])))[0]
    pairs = [[0, mate0], [k for k in range(1, N) if k != mate0]]
    half = 0 if rank in pairs[0] else 1
    pair, other = pairs[half], pairs[1 - half]
    place = pair.index(rank)
    partner, across = pair[1 - place], other[place]
    others = [(rank + d) % N for d in range(1, N)]
    QO, C, H = [], [], []

    def orders(r):
        first = 2 * half if MODES[r] == "pair" else 0
        known_first = [first, first + 1, 2 - first, 3 - first]
        QO[:] = known_first[2:] + known_first[:2] if MODES[r] == "pair" else known_first
        C[:] = [512 * q for q in known_first]
        H[:] = [C[0], C[2]]
        if MODES[r] == "own":
            mine = first = 2 * half + place
            QO[:] = [2 - 2 * half, 3 - 2 * half, mine ^ 1, mine]
            C[:] = [512 * q for q in (mine, mine ^ 1, mine ^ 2, mine ^ 3)]
            H[:] = [1024 * half, 1024 - 1024 * half]
    orders(0)

    op("y", lambda: g.sync.dma_start(T.nx32[:], T.nx[:]), writes=["nx32"], sem="ldnx", inc=16)
    op("s", lambda: S.dma_start(T.act32[:], T.act0[:]), writes=["act32"], sem="ldact", inc=16)
    op("y", lambda: g.sync.dma_start(T.rws[:], T.rw[:]), writes=["rws"], sem="ldrw", inc=16)
    op("s", lambda: S.dma_start(cap, T.cap[:]), writes=["cap"], sem="ldcap", inc=16)

    def iota(out, key, pattern, base, cm, flag=True):
        if flag:
            op("g", lambda: g.iota(out, pattern, base, cm, allow_small_or_imprecise_dtypes=True), writes=[key])
        else:
            op("g", lambda: g.iota(out, pattern, base, cm), writes=[key])

    def mark(out, key, n, pattern, fill, base, cm):
        op("g", lambda: g.affine_select(out, T.zeros[:, 0:n], pattern, A.not_equal, fill, base, cm),
           reads=["zeros"], writes=[key])

    def vts(out, in0, s1, s2, ops, reads, writes, banks=()):
        op("v", lambda: V.tensor_scalar(out, in0, s1, s2, *ops), reads=reads, writes=writes, banks=banks)

    def vcopy(out, in_, reads, writes):
        op("v", lambda: V.tensor_copy(out, in_), reads=reads, writes=writes)

    def vset(out, val, writes):
        op("v", lambda: V.memset(out, val), writes=writes)

    vset(T.zeros[:], 0.0, ["zeros"])
    iota(T.colmat[:], "colmat", [[-1, 16]], 0, 1)
    iota(T.g16[:], "g16", [[16, 8], [0, 16]], 0, 0)
    iota(T.pint[:, 0:1], "pint", [[0, 1]], 0, 1, False)
    mark(T.bmat[:, 1024:1536], "bm_hi", 512, [[-1, 4], [-16, 8], [0, 16]], 1.0, -8, 1)
    mark(T.bmat[:, 1536:2048], "bm_hj", 512, [[-1, 4], [-16, 8], [0, 16]], 1.0, -12, 1)
    iota(T.xrow[:], "xrow", [[1, 144]], 0, 0)
    iota(T.mtile[:], "mtile", [[16, 128]], 0, 0)
    vset(T.nf[:, 0:640:5], 0.0, ["nf0"])
    vset(T.nf[:, 4:640:5], 1.0, ["nf4"])
    vts(T.dnx[:, 0:640:5], T.zeros[:, 0:128], 0.0, None, [A.add], ["zeros"], ["dnx0"])
    columns = [
        lambda: vts(T.pint[:, 4:5], T.pint[:, 0:1], 15, None, [A.bitwise_and], ["pint"], ["pi"]),
        lambda: vcopy(icol, T.pint[:, 4:5], ["pi"], ["icol"]),
        lambda: vts(tcol, T.pint[:, 4:5], 8.0, 2.0, [A.is_ge, A.mult], ["pi"], ["tcol"]),
        lambda: vts(sgn, tcol, -1.0, None, [A.add], ["tcol"], ["sgn"]),
        lambda: vts(pbias, icol, -1031.5, sgn, [A.add, A.mult], ["icol", "sgn"], ["pb0"]),
        lambda: vts(pbias, pbias, 3072.0, None, [A.add], ["pb0"], ["pbias"]),
        lambda: vts(sgn16, sgn, 0.0625, None, [A.mult], ["sgn"], ["sgn16"]),
        lambda: vts(zcol, T.colmat[:, 0:1], icol, 15.0, [A.subtract, A.add], ["colmat", "icol"], ["zcol"])]
    for i in range(8):
        vts(T.bmat[:, 128 * i:128 * i + 128], T.g16[:], T.colmat[:, i:i + 1], None, [A.is_equal], ["g16", "colmat"], ["bm%d" % i])
        if i % 2:
            columns.pop(0)()
    BM = ["bm_hi", "bm_hj"] + ["bm%d" % i for i in range(8)]
    for a in range(1, 4):
        vts(T.nf[:, a:640:5], T.act32[:], float(a), None, [A.is_lt], ["act32"], ["nf%d" % a])
    vcopy(T.dnx[:, 4:640:5], T.nx32[:, 384:512], ["nx32"], ["dnx4"])
    for a in range(1, 4):
        op("v", lambda: V.tensor_tensor(T.dnx[:, a:640:5], T.nx32[:, 128 * a - 128:128 * a], T.nx32[:, 128 * a:128 * a + 128], A.subtract),
           reads=["nx32"], writes=["dnx%d" % a])
    columns.pop(0)()
    op("v", lambda: V.tensor_tensor_scan(T.unx[:], T.dnx[:], T.nf[:], 0.0, A.add, A.mult),
       reads=K("dnx", 0, 5, 1) + K("nf", 0, 5, 1), writes=["unx"])
    while columns:
        columns.pop(0)()

    def lst0(r, lo, hi):
        return T.l0[:, 128 * r + lo // 16:128 * r + hi // 16]

    def lst(k, lo, hi):
        return T.lists[:, 128 * (k - 1) + lo // 16:128 * (k - 1) + hi // 16]

    def L(k, lo, hi):
        return K("L%s_" % k, lo, hi, 512)

    def X(b, lo=0, hi=512, step=1):
        return T.xx[:, 512 * b + lo:512 * b + hi:step]

    def pieces(e, out, b, writes):
        if e == "v":
            vts(out, X(b), sgn, pbias, [A.mult, A.add], ["sgn", "pbias"], writes, ["x%d" % b])
        else:
            op("s", lambda: S.activation(out, X(b), F.Identity, bias=pbias, scale=sgn), reads=["sgn", "pbias"], writes=writes, banks=["x%d" % b])

    def trow_pe(q):
        def fn():
            for i in range(16):
                ins = P.matmul(X(q, i, 512, 16), T.bmat[:, 128 * i:128 * i + 128], T.unx[:, 160 * q + 4:160 * q + 160:5], True, True)
            return ins
        op("p", fn, reads=["unx"] + BM, banks=["x%d" % q])

    def trow_ev(q, e):
        pieces(e, T.ta[:, 512 * q:512 * q + 512], q, K("ta", 512 * q, 512 * q + 512))

    for q in range(4):
        trow_pe(q)
    vcopy(lst(1, 0, 2048), T.unx[:, 4:640:5], ["unx"], L(1, 0, 2048))
    trow_ev(0, "s")
    trow_ev(1, "s")
    vts(T.tmpf[:, 0:128], T.act32[:], 2048.0, icol, [A.mult, A.add], ["act32", "icol"], ["t0"])
    vts(T.zmat[:], T.xrow[:], zcol, sgn16, [A.is_equal, A.mult], ["xrow", "zcol", "sgn16"], ["zmat"])
    op("v", lambda: V.tensor_tensor(T.tmpf[:, 128:256], T.tmpf[:, 0:128], T.mtile[:], A.add), reads=["t0", "mtile"], writes=["t1"])
    vts(cap16, cap, 0.0625, None, [A.mult], ["cap"], ["cap16"])
    trow_ev(2, "v")
    trow_ev(3, "s")
    vcopy(lst0(0, 0, 2048), T.tmpf[:, 128:256], ["t1"], L("a0", 0, 2048))
    vcopy(T.nxh[:], T.nx32[:], ["nx32"], ["nxh"])
    vts(T.sel[:], T.xrow[:, 15:128:16], zcol, None, [A.is_equal], ["xrow", "zcol"], ["sel"])
    vcopy(T.nxu[:], T.nxh[:], ["nxh"], ["nxu"])
    op("g", lambda: g.affine_select(T.sumrw[:], T.zeros[:], [[0, 512]], A.is_gt, 0.0, 1, 0), reads=["zeros"], writes=K("sumrw", 0, 4, 1))
    mark(T.ident[:], "ident", 128, [[-1, 128]], 1.0, 0, 1)
    mark(T.nident[:], "nident", 128, [[-1, 128]], -1.0, 0, 1)
    mark(T.prm[:, 0:128], "prm0", 128, [[1, 32], [32, 4]], 512.0, 0, -1)
    mark(T.prm[:, 128:256], "prm", 128, [[1, 32], [-32, 4]], 512.0, 96, -1)
    if NS < 512:
        vts(T.cols[:, 0:1], T.colmat[:, 0:1], 32.0 + NS // 16, None, [A.is_ge], ["colmat"], ["vmask"])
    mark(T.reset[:], "reset", 256, [[0, 64], [1, 4]], float(2 ** 23), 0, 0)
    iota(T.ones[0:1, :], "ones", [[0, 128]], 1, 0)
    iota(T.kc1[0:1, :], "kc1", [[1, 128], [0, 4]], 0, 0)
    iota(T.kc2[0:1, :], "kc2", [[0, 64], [128, 4]], 0, 0)

    def shadow(name, lo, hi, by_dma):
        if by_dma:
            op("y", lambda: g.sync.dma_start(T.dc[:, lo:hi], T[name][:, lo:hi]), reads=K(name, lo, hi), writes=K("dc", lo, hi),
               sem="sh%d" % (lo // 256), inc=16)
        else:
            op("g", lambda: g.affine_select(T.dc[:, lo:hi], T[name][:, lo:hi], [[0, hi - lo]], A.is_gt, 0.0, 1, 0),
               reads=K(name, lo, hi), writes=K("dc", lo, hi))

    def dfirst(e, r, lo, hi):
        win = T.rws[:, 0:8192].indirect(lst0(r, lo, hi))
        if e == "v":
            vts(T.da[:, lo:hi], win, -1.0, cap16, [A.mult, A.add], ["rws", "cap16"] + L("a%d" % r, lo, hi), K("da", lo, hi))
        else:
            op("s", lambda: S.activation(T.da[:, lo:hi], win, F.Identity, bias=cap16, scale=-1.0),
               reads=["rws", "cap16"] + L("a%d" % r, lo, hi), writes=K("da", lo, hi))

    def tfirst(r, lo, hi):
        vcopy(T.ta[:, lo:hi], T.nxrow[:, 0:8192].indirect(lst0(r, lo, hi)), K("nxrow", 0, 16, 1) + L("a%d" % r, lo, hi), K("ta", lo, hi))

    def ext(name, lo, hi, b):
        def fn():
            for i in range(16):
                ins = P.matmul(T[b][:, 0:(hi - lo) // 16], T.zmat[:, 15 - i:143 - i], T[name][:, lo + i:hi:16], i == 0, i == 15)
            return ins
        op("p", fn, reads=K(name, lo, hi) + ["zmat"], banks=[b])

    def conv(k, lo, hi, b):
        vts(lst(k, lo, hi), T[b][:, 0:(hi - lo) // 16], 1024.0, None, [A.add], [], L(k, lo, hi), [b])

    def exth(name, h):
        ext(name, H[h], H[h] + 1024, "e%d" % h)

    def convh(k, h):
        conv(k, H[h], H[h] + 1024, "e%d" % h)

    def dstep(src, dst, k, lo, hi):
        op("v", lambda: V.tensor_tensor(T[dst][:, lo:hi], T[src][:, 0:2048].indirect(lst(k, lo, hi)), T.dc[:, lo:hi], A.add),
           reads=K(src, 0, 2048) + L(k, lo, hi) + K("dc", lo, hi), writes=K(dst, lo, hi))

    def dgather(src, k, lo, hi, j):
        g0, n, b = 512 * j, hi - lo, "x%d" % j

        def fn():
            P.matmul(X(j, 0, n), T.ident[:], T[src][:, lo:hi], True, False)
            return None
        op("s", lambda: S.activation(T.gbuf[:, g0:g0 + n], T[src][:, 0:2048].indirect(lst(k, lo, hi)), F.Copy),
           reads=K(src, 0, 2048) + L(k, lo, hi), writes=["g%d" % j])
        op("p", fn, reads=K(src, lo, hi) + ["ident"], banks=[b], inc=0)
        op("p", lambda: P.matmul(X(j, 0, n), T.ident[:], T.gbuf[:, g0:g0 + n], False, True), reads=K(src, lo, hi) + ["g%d" % j], banks=[b])

    def dback(dst, lo, hi, j):
        b = "x%d" % j
        op("s", lambda: S.activation(T[dst][:, lo:hi], X(j, 0, hi - lo), F.Copy), writes=K(dst, lo, hi), banks=[b])

    def tstep(e, src, dst, k, lo, hi):
        win = T[src][:, 0:2048].indirect(lst(k, lo, hi))
        op(e, (lambda: S.activation(T[dst][:, lo:hi], win, F.Copy)) if e == "s" else (lambda: V.tensor_copy(T[dst][:, lo:hi], win)),
           reads=K(src, 0, 2048) + L(k, lo, hi), writes=K(dst, lo, hi))

    def rwsum(j):
        b = "s%d" % (j % 2)

        def fn():
            for a in range(2 if j % 2 and NS == 512 else 3):
                c0, p0 = a * 2048 + 512 * QO[j], 32 * (3 - a if j % 2 else a)
                for i in range(16):
                    ins = P.matmul(T[b][p0:p0 + 32, i:128:16], T.rws[:, c0 + i:c0 + 512:16], T.sel[:], True, True)
            return ins
        op("p", fn, reads=["rws", "sel"], banks=[b])

    def rwback(j):
        b = "s%d" % (j % 2)
        lo, hi = (64, 128) if j % 2 else (0, 96)
        op("v", lambda: V.tensor_copy(T.sumrw[lo:hi, 128 * j:128 * j + 128], T[b][lo:hi, 0:128]), writes=["sumrw%d" % j], banks=[b])
        if j % 2 and NS < 512:
            vts(T.sumrw[32:64, 128 * j:128 * j + 128], T[b][32:64, 0:128], T.cols[32:64, 0:1], None, [A.mult], ["vmask"], ["sumrw%d" % j], [b])

    def engines(ranks):
        m = -1
        for k in ranks:
            m &= topo.mask(core, T.cores[k])
        return m

    def write(ranks, src, dst, sem, reads, extra=()):
        m = engines(ranks)
        ids = [DstId(rid=topo.addr(T.cores[k])[0], pnc=topo.addr(T.cores[k])[1]) for k in ranks]

        def fn():
            g.remote_dma_fused([RemoteDMATransfer(dst_ids=ids, dma_engine_mask=m, remote_sem=T.sem[sem], srcs=[src], dsts=[dst] * len(ids))],
                               local_sem=T.sem.sent)
        return op("g", fn, reads=reads, extra=extra, sem="sent", inc=bin(m).count("1"))

    def landed(name, k, ranks):
        m = -1
        for d in ranks:
            m &= topo.mask(T.cores[k], T.cores[d])
        return (name, bin(m).count("1"), "x", {})

    def slot(r, j, n=1):
        return T.land[:, (r * 16 + j) * 128:(r * 16 + j + n) * 128]

    def qv(j, a):
        lo = NS if a == 2 and j % 2 else 0
        if lo == 512:
            return
        y0, c0, n = 2048 * j + 512 * (3 - a if j % 2 else a) + lo, 2048 * a + 512 * QO[j] + lo, 512 - lo
        op("v", lambda: V.tensor_tensor(T.ybuf[:, y0:y0 + n], T.da[:, 0:2048].indirect(T.nxu[:, c0 // 16:(c0 + n) // 16]),
                                        T.rws[:, c0:c0 + n], A.max),
           reads=K("da", 0, 2048) + ["nxu", "rws"], writes=["yv%d%d" % (j, a)])

    def spart(h, t):
        c0 = 2048 * (3 if t < 2 else 2) + 512 * QO[2 * h + min(t, 1)]
        return c0, 512 if t < 2 else NS, (3 * h + t) % 4

    def qsub(h, t):
        c0, n, b = spart(h, t)

        def fn():
            P.matmul(X(b, 0, n), T.nident[:], T.rws[:, c0:c0 + n], True, False)
            return None
        op("p", fn, reads=["rws", "nident"], banks=["x%d" % b], inc=0)

    def qg(h, t0, t1):
        if t1 - t0 == 2 and QO[2 * h + 1] != QO[2 * h] + 1:
            qg(h, t0, t0 + 1)
            qg(h, t0 + 1, t1)
            return
        c0, g0 = spart(h, t0)[0], 512 * (3 * h + t0)
        n = sum(spart(h, t)[1] for t in range(t0, t1))
        op("s", lambda: S.activation(T.gbuf[:, g0:g0 + n], T.da[:, 0:2048].indirect(T.nxu[:, c0 // 16:(c0 + n) // 16]), F.Copy),
           reads=K("da", 0, 2048) + ["nxu"], writes=K("g", 3 * h + t0, 3 * h + t1, 1))
        for t in range(t0, t1):
            c0, n, b = spart(h, t)
            g0 = 512 * (3 * h + t)
            op("p", lambda: P.matmul(X(b, 0, n), T.ident[:], T.gbuf[:, g0:g0 + n], False, True),
               reads=["g%d" % (3 * h + t), "ident"], banks=["x%d" % b])

    def qr(h, t0, t1):
        y0, n = 4096 * h + 1536 + 512 * t0, sum(spart(h, t)[1] for t in range(t0, t1))
        op("s", lambda: S.activation(T.ybuf[:, y0:y0 + n], X(spart(h, t0)[2], 0, n), F.Relu), writes=K("ys%d" % h, t0, t1, 1),
           banks=["x%d" % spart(h, t)[2] for t in range(t0, t1)])

    def qsum(j):
        b = "s%d" % (j % 2)

        def fn():
            for i in range(16):
                ins = P.matmul(T[b][:, i:128:16], T.ybuf[:, 2048 * j + i:2048 * j + 2048:16], T.sel[:], True, True)
            return ins
        op("p", fn, reads=["yv%d%d" % (j, a) for a in range(3)] + ["ys%d%d" % (j // 2, t) for t in ((1, 2) if j % 2 else (0,))] + ["sel"],
           banks=[b])

    def qcv(r, j):
        b, c = "s%d" % (j % 2), j % 2
        out = slot(r, 8 + j) if j < 2 else slot(r, 4 * c + 3 * place)
        if MODES[r] == "all":
            out = slot(r, 4 * rank + j)
        if MODES[r] == "own":
            out = slot(r, 8 + j)
        op("v", lambda: V.tensor_tensor(out, T[b][:, 0:128], T.sumrw[:, 128 * j:128 * j + 128], A.subtract),
           reads=["sumrw%d" % j], writes=["own%d%d" % (r, j)], banks=[b])
        if MODES[r] == "own":
            if j < 2:
                write([other[j]], out, slot(r, place), "far%d%d" % (r, place), ["own%d%d" % (r, j)])
            elif j == 2:
                write([partner], out, slot(r, 2), "near%d0" % r, ["own%d%d" % (r, j)])
        elif MODES[r] == "all":
            if c == 1:
                out = slot(r, 4 * rank + j - 1, 2)
                write(others, out, out, "far%d%d" % (r, j // 2), ["own%d%d" % (r, j - 1), "own%d%d" % (r, j)])
        elif j < 2:
            write([other[j]], out, slot(r, 4 * j + 1 + place), "far%d%d" % (r, place), ["own%d%d" % (r, j)])
        elif c == place:
            out = slot(r, 4 * c + place, 3)
            write([partner], out, out, "near%d%d" % (r, c), ["own%d%d" % (r, j)], far(r))
        else:
            write([partner], out, out, "near%d%d" % (r, c), ["own%d%d" % (r, j)])

    def far(r):
        return [landed("far%d%d" % (r, p), other[p], [rank]) for p in range(2)]

    def keys(r, c, part):
        b = "e%d" % c
        out = T[b][:, 0:128]
        here = [3 * place] + ([1, 2] if c == place else [])
        todo = here if part == 0 else [j for j in range(4) if j not in here]

        def fn():
            if part == 0:
                P.matmul(out, T.ones[0:1, :], T.kc1[0:1, C[c] // 4:C[c] // 4 + 128], True, False)
                P.matmul(out, T.ones[0:1, :], T.kc2[0:1, 0:128], False, False)
            for j in todo:
                ins = P.matmul(out, slot(r, 4 * c + j), T.prm[:, 128 * c:128 * c + 128], False, part == 1 and j == todo[-1])
            return ins if part else None
        if part == 0:
            op("p", fn, reads=["ones", "kc1", "kc2", "prm", "own%d%d" % (r, 2 + c)], banks=[b], extra=far(r) if c == place else [], inc=0)
        else:
            op("p", fn, banks=[b], extra=[landed("near%d%d" % (r, c), partner, [rank])])

    def keys_own(r, part):
        out = T.e0[:, 0:128]

        def fn():
            if part == 0:
                P.matmul(out, T.ones[0:1, :], T.kc1[0:1, C[0] // 4:C[0] // 4 + 128], True, False)
                P.matmul(out, T.ones[0:1, :], T.kc2[0:1, 0:128], False, False)
                for j in range(2):
                    P.matmul(out, slot(r, j), T.prm[:, 128 * place:128 * place + 128], False, False)
            elif part == 1:
                P.matmul(out, slot(r, 11), T.prm[:, 128:256], False, False)
            else:
                return P.matmul(out, slot(r, 2), T.prm[:, 0:128], False, True)
            return None
        op("p", fn, reads=["ones", "kc1", "kc2", "prm"] + (["own%d3" % r] if part == 1 else []), banks=["e0"],
           extra=[far(r), [], [landed("near%d0" % r, partner, [rank])]][part], inc=part // 2)

    def choose(r, c):
        b, lo, hi = "e%d" % c, C[c], C[c] + 512
        if MODES[r] == "own":
            rest = [partner, across, other[1 - place]]
            sc, ki, km = T.scan[:, 0:128], T.ki[:, 0:32], T.km[:, 0:32]
            op("v", lambda: V.tensor_tensor_scan(sc, T.reset[:, 0:128], T[b][:, 0:128], 0.0, A.add, A.min), reads=["reset"], writes=["scan0"], banks=[b])
            vcopy(ki, T.scan[:, 3:128:4], ["scan0"], ["ki0"])
            if r < RO - 1:
                out, key = lst0(r + 1, lo, hi), L("a%d" % (r + 1), lo, hi)
                vts(km, ki, 511, None, [A.bitwise_and], ["ki0"], ["km0"])
                vts(out, km, 16.0, icol, [A.mult, A.add], ["km0", "icol"], key)
            else:
                out, key = T.yas[:, lo // 16:hi // 16], ["yas0"]
                vts(km, ki, 7, 3, [A.arith_shift_right, A.bitwise_and], ["ki0"], ["km0"])
                vcopy(out, km, ["km0"], key)
            write(rest, out, out, "act%d%d" % (r, rank), key)
            for j in range(1, 4):
                for name in (L("a%d" % (r + 1), C[j], C[j] + 512) if r < RO - 1 else ["yas%d" % j]):
                    lastw[name] = landed("act%d%d" % (r, rest[j - 1]), rest[j - 1], [k for k in range(N) if k != rest[j - 1]])
            return
        sc, ki, km = T.scan[:, 128 * c:128 * c + 128], T.ki[:, 32 * c:32 * c + 32], T.km[:, 32 * c:32 * c + 32]
        op("v", lambda: V.tensor_tensor_scan(sc, T.reset[:, 0:128], T[b][:, 0:128], 0.0, A.add, A.min), reads=["reset"], writes=["scan%d" % c], banks=[b])
        vcopy(ki, T.scan[:, 128 * c + 3:128 * c + 128:4], ["scan%d" % c], ["ki%d" % c])
        if r < RO - 1:
            out, key = lst0(r + 1, lo, hi), L("a%d" % (r + 1), lo, hi)
            vts(km, ki, 511, None, [A.bitwise_and], ["ki%d" % c], ["km%d" % c])
            vts(out, km, 16.0, icol, [A.mult, A.add], ["km%d" % c, "icol"], key)
            write([across], out, out, "chosen%d%d" % (r, c), key)
            for name in L("a%d" % (r + 1), C[2 + c], C[2 + c] + 512):
                lastw[name] = landed("chosen%d%d" % (r, c), across, [rank])
        else:
            vts(km, ki, 7, 3, [A.arith_shift_right, A.bitwise_and], ["ki%d" % c], ["km%d" % c])
            vcopy(T.yas[:, lo // 16:hi // 16], km, ["km%d" % c], ["yas%d" % c])
            if c == 1:
                out = T.yas[:, H[0] // 16:H[0] // 16 + 64]
                write([across], out, out, "chosen%d%d" % (r, c), ["yas0", "yas1"])
                lastw["yas2"] = landed("chosen%d%d" % (r, c), across, [rank])

    def keys_all(r, h, part):
        b = "e%d" % h
        todo = [(k, q) for k in ([rank] if part == 0 else others) for q in range(2)]

        def fn():
            if part == 0:
                P.matmul(T[b][:, 0:256], T.ones[0:1, :], T.kc1[0:1, 256 * h:256 * h + 256], True, False)
                P.matmul(T[b][:, 0:256], T.ones[0:1, :], T.kc2[0:1, :], False, False)
            for k, q in todo:
                ins = P.matmul(T[b][:, 128 * q:128 * q + 128], slot(r, 4 * k + 2 * h + q), T.prm[:, 128 * q:128 * q + 128], False,
                               part == 1 and (k, q) == todo[-1])
            return ins if part else None
        if part == 0:
            op("p", fn, reads=["ones", "kc1", "kc2", "prm", "own%d%d" % (r, 2 * h), "own%d%d" % (r, 2 * h + 1)], banks=[b], inc=0)
        else:
            a = landed("far%d%d" % (r, h), others[0], [rank])
            op("p", fn, banks=[b], extra=[(a[0], a[1] * (N - 1), "x", {})])

    def choose_all(r, c):
        b, lo, hi = "e%d" % c, 1024 * c, 1024 * c + 1024
        sc, ki, km = T.scan[:, 256 * c:256 * c + 256], T.ki[:, 64 * c:64 * c + 64], T.km[:, 64 * c:64 * c + 64]
        op("v", lambda: V.tensor_tensor_scan(sc, T.reset[:], T[b][:, 0:256], 0.0, A.add, A.min), reads=["reset"], writes=["scan%d" % c], banks=[b])
        vcopy(ki, T.scan[:, 256 * c + 3:256 * c + 256:4], ["scan%d" % c], ["ki%d" % c])
        if r < RO - 1:
            out, key = lst0(r + 1, lo, hi), L("a%d" % (r + 1), lo, hi)
            vts(km, ki, 511, None, [A.bitwise_and], ["ki%d" % c], ["km%d" % c])
            vts(out, km, 16.0, icol, [A.mult, A.add], ["km%d" % c, "icol"], key)
        else:
            vts(km, ki, 7, 3, [A.arith_shift_right, A.bitwise_and], ["ki%d" % c], ["km%d" % c])
            vcopy(T.yas[:, lo // 16:hi // 16], km, ["km%d" % c], ["yas%d" % c])

    def rows_pe(i):
        b = (i + 2 - EARLY) % 4
        op("p", lambda: P.matmul(X(b), T.bmat[:, 128 * i:128 * i + 128], T.nxh[:], True, True), reads=["nxh"] + BM, banks=["x%d" % b])

    def rows_ev(i):
        pieces("v" if i in ROWS_ON_V else "s", T.nxrow[:, i:8192:16], (i + 2 - EARLY) % 4, ["nxrow%d" % i])

    ds, ts = ["da", "db"], ["ta", "tb"]

    def helped(k, small_first, pending=None, last=True):
        s0, s1 = ds[(k - 1) % 2], ds[k % 2]
        y, z = (C[3] + 256, C[3]) if k % 2 == 0 else (C[3], C[3] + 256)
        parts = [(C[0], C[0] + 512, 2 * (k % 2)), (y, y + 256, 2 * (k % 2) + 1)]
        if last and not small_first and YS < 256:
            dgather(s0, k, *parts[0])
            dstep(s0, s1, k, C[1], C[1] + 512)
            pending()
            if YS:
                dgather(s0, k, C[3] + 512 - YS, C[3] + 512, parts[1][2])
            dback(s1, *parts[0])
            dstep(s0, s1, k, C[2], C[2] + 512)
            dstep(s0, s1, k, C[3], C[3] + 512 - YS)
            if YS:
                dback(s1, C[3] + 512 - YS, C[3] + 512, parts[1][2])
            return
        if small_first:
            parts.reverse()
        dgather(s0, k, *parts[0])
        dstep(s0, s1, k, C[1], C[1] + 512)
        if not last:
            shadow(s1, C[1], C[1] + 512, False)
        if pending:
            pending()
        dgather(s0, k, *parts[1])
        dback(s1, *parts[0])
        if small_first and not last:
            shadow(s1, y, y + 256, True)
        dstep(s0, s1, k, C[2], C[2] + 512)
        if not last:
            shadow(s1, C[2], C[2] + 512, False)
        dstep(s0, s1, k, z, z + 256)
        dback(s1, *parts[1])
        if not small_first and not last:
            shadow(s1, y, y + 256, True)

    def beside(k, kt, kh, early=None):
        s0, s1 = ds[(k - 1) % 2], ds[k % 2]
        t0, t1 = ts[(kt - 1) % 2], ts[kt % 2]
        order = (1, 0, 2, 3) if (kh - k) % 2 else (0, 1, 3, 2)
        z = C[3] + 256 * (kh % 2)
        for h in range(2):
            tstep("s", t0, t1, kt, H[h], H[h] + 1024)
            for p in range(2):
                j = order[2 * h + p]
                if k == 0:
                    dfirst("s" if R0S and (h, p) == (0, 1) else "v", 0, C[j], C[j] + 512)
                else:
                    dstep(s0, s1, k, C[j], C[j] + 512)
                if k + 1 < kh:
                    shadow(s1, C[j], C[j] + 512, p == 0)
                elif j in (1, 2):
                    shadow(s1, C[j], C[j] + 512, j == 1)
                elif j == 3:
                    shadow(s1, z, z + (512 - YS if kh == 4 else 256), False)
                if h == 0 and p == CONV[0]:
                    (early or (lambda: convh(kt, 1)))()
                if h == 1 and p == (CONV[1] if k else 1):
                    convh(kt + 1, 0)
            exth(t1, h)
            if k + h > 0:
                rwnext()

    def rwnext():
        if sums:
            j = sums.pop(0)
            if j > 1:
                rwback(j - 2)
            if j < 4:
                rwsum(j)

    sums = list(range(6))
    for k in range(1, SHARED + 1):
        t0, t1 = ts[(k - 1) % 2], ts[k % 2]
        tstep("v", t0, t1, k, C[0], C[0] + 512)
        tstep("s", t0, t1, k, C[1], C[1] + 512)
        if k > 1:
            convh(k, 1)
        exth(t1, 0)
        tstep("v", t0, t1, k, C[2], C[2] + 512)
        tstep("s", t0, t1, k, C[3], C[3] + 512)
        convh(k + 1, 0)
        exth(t1, 1)
    kh = 3 - SHARED
    if AHEAD:
        for h in range(2):
            tstep("s", "ta", "tb", 1, H[h], H[h] + 1024)
            exth("tb", h)
        for e, j, by_dma in R0PLAN:
            dfirst(e, 0, C[j], C[j] + 512)
            shadow("da", C[j], C[j] + 512, by_dma)
        convh(2, 0)
        rwnext()
        beside(1, 2, 3)
        for i in range(EARLY):
            rows_pe(i)
        beside(2, 3, 3)
        for i in range(EARLY):
            rows_ev(i)
    for k in range(0 if AHEAD else kh):
        if k == 0:
            if SHARED:
                convh(SHARED + 1, 1)
            beside(k, SHARED + 1 + k, kh, lambda: None)
        else:
            beside(k, SHARED + 1 + k, kh)
    for k in range(kh, 5):
        helped(k, k < 4, (lambda: convh(4, 1)) if k == kh else (lambda: None), k == 4)
        rwnext()
    while sums:
        rwnext()

    for r in range(RO):
        if r > 0:
            beside(1, 1, 4)
            beside(2, 2, 4)
            beside(3, 3, 4)
            helped(4, False, lambda: convh(4, 1))
        orders(r)

        for h, t in ((0, 0), (0, 1), (0, 2), (1, 0)):
            qsub(h, t)
        for h in range(2):
            j = 2 * h
            qv(j, 0)
            if h == 1:
                qsum(1)
                qcv(r, 1)
            if SOPS[h] == 4:
                qg(h, 0, 2)
                qg(h, 2, 3)
                qr(h, 0, 1)
            else:
                qg(h, 0, 1)
                qg(h, 1, 2)
                qr(h, 0, 1)
            qv(j, 1)
            qv(j, 2)
            if h == 0:
                qsub(1, 1)
            qsum(j)
            if SOPS[h] > 4:
                qg(h, 2, 3)
            qv(j + 1, 1)
            if QCV[h] == 0:
                qcv(r, j)
            qv(j + 1, 0)
            if QCV[h] == 1:
                qcv(r, j)
            qv(j + 1, 2)
            if h == 1 and r == 0:
                rows_pe(EARLY)
                rows_pe(EARLY + 1)
            if SOPS[h] < 6:
                qr(h, 1, 3)
            else:
                qr(h, 1, 2)
                qr(h, 2, 3)
            if h == 0:
                qsub(1, 2)
        qsum(3)
        if r == 0:
            rows_ev(EARLY)
            rows_ev(EARLY + 1)
            for i in range(EARLY + 2, EARLY + 4):
                rows_pe(i)
                rows_ev(i)
        if r == RO - 1:
            vts(T.db[:, 1024:2048], T.da[:, 1024:2048], 0.0, -1.0, [A.max, A.mult], K("da", 1024, 2048), K("db", 1024, 2048))
            op("s", lambda: S.activation(T.db[:, 0:1024], T.da[:, 0:1024], F.Relu), reads=K("da", 0, 1024), writes=K("db", 0, 1024))
            op("s", lambda: S.activation(T.yrs[:, 1024:2048], T.db[:, 1024:2048], F.Identity, bias=cap),
               reads=K("db", 1024, 2048) + ["cap"], writes=["yrs1"])
        qcv(r, 3)
        if r == RO - 1:
            vts(T.yrs[:, 0:1024], T.db[:, 0:1024], -1.0, cap, [A.mult, A.add], K("db", 0, 1024) + ["cap"], ["yrs0"])
            for h in range(2):
                op("y", lambda: g.sync.dma_start(T.yr[:, 1024 * h:1024 * h + 1024], T.yrs[:, 1024 * h:1024 * h + 1024]),
                   reads=["yrs%d" % h], sem="st", inc=16)

        def rows(lo, hi):
            for i in range(max(lo, EARLY + 4), hi if r == 0 else lo):
                rows_pe(i)
                rows_ev(i)

        def start(j):
            lo, hi = C[j], C[j] + 512
            tfirst(r + 1, lo, hi)
            dfirst("s", r + 1, lo, hi)
            shadow("da", lo, hi, SH0[j])

        if MODES[r] == "all":
            rows(4, 16)
            keys_all(r, 0, 0)
            keys_all(r, 0, 1)
            keys_all(r, 1, 0)
            choose_all(r, 0)
            if r < RO - 1:
                start(0)
                start(1)
                ext("ta", 0, 1024, "e0")
            keys_all(r, 1, 1)
            if r < RO - 1:
                conv(1, 0, 1024, "e0")
            choose_all(r, 1)
            if r < RO - 1:
                tfirst(r + 1, 1024, 2048)
                for lo in (1024, 1536):
                    dfirst("s", r + 1, lo, lo + 512)
                    shadow("da", lo, lo + 512, False)
                ext("ta", 1024, 2048, "e1")
            else:
                op("s", lambda: S.dma_start(T.ya[:], T.yas[:]), reads=["yas0", "yas1"], sem="st", inc=16)
            continue
        if MODES[r] == "own":
            keys_own(r, 0)
            keys_own(r, 1)
            rows(4, ROWS[0])
            keys_own(r, 2)
            choose(r, 0)
            rows(ROWS[0], 16)
        else:
            rows(4, ROWS[0])
            keys(r, 0, 0)
            keys(r, 0, 1)
            keys(r, 1, 0)
            choose(r, 0)
            rows(ROWS[0], ROWS[1])
            keys(r, 1, 1)
            choose(r, 1)
            rows(ROWS[1], 16)
        if r < RO - 1:
            start(0)
            start(1)
            ext("ta", H[0], H[0] + 1024, "e0")
            start(2)
            conv(1, H[0], H[0] + 1024, "e0")
            start(3)
            exth("ta", 1)
        else:
            op("s", lambda: S.dma_start(T.ya[:], T.yas[:]), reads=["yas0", "yas1", "yas2", "yas3"], sem="st", inc=16)

    g.sync.wait_ge(T.sem.st, count["st"])
    for s in ("cg", "sent", "cp", "cs", "cv"):
        g.wait_ge(T.sem[s], count[s])
